import numpy as np
import ml_dtypes


def mxq(x, axis, fmt="e4m3"):
    dtype, down = {"e4m3": (ml_dtypes.float8_e4m3fn, 7), "e5m2": (ml_dtypes.float8_e5m2, 14)}[fmt]
    v = np.moveaxis(np.asarray(x, np.float32).astype(ml_dtypes.bfloat16).astype(np.float64), axis, -1)
    blocks = v.reshape(v.shape[:-1] + (-1, 32))
    amax = np.abs(blocks).max(-1, keepdims=True)
    byte = np.maximum(np.where(amax > 0, np.frexp(amax)[1] - 1 + 127, 0) - down, 1)
    scale = np.exp2(byte - 127.0)
    codes = (blocks / scale).astype(np.float32).astype(dtype).astype(np.float64)
    return np.moveaxis((codes * scale).reshape(v.shape), -1, axis)


WIDE = False


def mx_kscale(k):
    if not WIDE:
        return np.ones(k)
    levels = np.array([10, -10, 5, -5, 0])
    if k % 512:
        return np.exp2(np.random.permutation(np.resize(levels, k // 32))).repeat(32)
    a = np.empty((k // 512, 16))
    for p in range(k // 512):
        a[p, :8] = np.random.permutation(np.resize(levels, 8))
        for g in range(8):
            far = levels[np.abs(levels - a[p, g]) >= 10]
            a[p, g + 8] = far[np.random.randint(len(far))]
    return np.exp2(a.ravel()).repeat(32)


def f64(x):
    return np.asarray(x).astype(np.float64)


def striped(idx):
    return np.tile(np.asarray(idx).reshape(-1, 16).T, (8, 1)).astype(np.uint16)


def unstriped(offs):
    return offs[:16].T.reshape(-1).astype(np.int64)


E2M1 = np.array([0.0, 0.5, 1.0, 1.5, 2.0, 3.0, 4.0, 6.0, -0.0, -0.5, -1.0, -1.5, -2.0, -3.0, -4.0, -6.0])


def pack_weight(w, fmt):
    k, n = w.shape
    w = f64(np.asarray(w, np.float32).astype(ml_dtypes.bfloat16)).reshape(k // 32, 32, n)
    amax = np.abs(w).max(1)
    if fmt == "e4m3":
        byte = np.frexp(amax)[1] - 1 + 127 - 7
    else:
        mant, ex = np.frexp(amax / 6.0)
        byte = np.where(mant > 0.5, ex, ex - 1) + 127
    byte = np.clip(np.where(amax > 0, byte, 1), 1, 254)
    scaled = (w * np.exp2(127.0 - byte)[:, None, :]).reshape(k, n).astype(np.float32)
    by_word = np.ascontiguousarray(scaled.reshape(k // 512, 128, 4, n).transpose(0, 1, 3, 2))
    if fmt == "e4m3":
        words = by_word.astype(ml_dtypes.float8_e4m3fn).view(np.uint8)
    else:
        c = by_word.astype(ml_dtypes.float4_e2m1fn).view(np.uint8) & 0xF
        words = (c[..., 0::2] | (c[..., 1::2] << 4)).reshape(k // 512, 128, 2 * n)
    return np.ascontiguousarray(words), np.ascontiguousarray(byte.astype(np.uint8).reshape(k // 512, 16, n))


def unpack_weight(words, scales, fmt):
    g, _, n = scales.shape
    words = np.ascontiguousarray(words).reshape(g, 128, n, -1)
    if fmt == "e4m3":
        vals = words.view(ml_dtypes.float8_e4m3fn).astype(np.float64)
    else:
        nib = np.empty((g, 128, n, 4), np.uint8)
        nib[..., 0::2] = words & 0xF
        nib[..., 1::2] = words >> 4
        vals = E2M1[nib]
    vals = vals * np.repeat(np.exp2(scales.astype(np.float64) - 127.0), 8, axis=1)[..., None]
    return vals.transpose(0, 1, 3, 2).reshape(g * 512, n)


B, N, T, D, DV, NQ = 1, 512, 1024, 512, 128, 256


def setup_inputs():
    n = np.random.standard_normal
    idx = np.sort(np.random.permutation(T)[:B * N].reshape(B, N), axis=1).reshape(-1)
    s = mx_kscale(D)[:, None]
    u = np.ones(T)
    u[idx] = mx_kscale(B * N)
    r = np.random.uniform(0.5, 2.0, T)
    k = n((D, T)) / s
    v = n((DV, T)) / (u * r)
    kp = pack_weight(k, "e4m3")
    return {
        "qT": (n((B, D, NQ)) * s * (0.80 / np.sqrt(D))).astype(np.float32),
        "k_words": kp[0],
        "k_scales": kp[1],
        "vT": v.astype(np.float32),
        "vs": np.tile(u * r, (128, 1)).astype(np.float32),
        "kb": np.tile(n(T), (128, 1)).astype(np.float32),
        "offs": striped(idx),
    }


def reference(qT, k_words, k_scales, vT, vs, kb, offs):
    idx = unstriped(offs)
    k = unpack_weight(k_words, k_scales, "e4m3")
    v = f64(vT)
    pick = lambda x: x[:, idx].reshape(x.shape[0], B, N).transpose(1, 0, 2)
    q = f64(qT)
    score = mxq(q, 1, "e4m3").transpose(0, 2, 1) @ pick(k)
    score = score + pick(f64(kb))[:, :1, :]
    m = score.max(-1, keepdims=True)
    p = np.exp(score - m)
    total = p.sum(-1, keepdims=True)
    w = p * pick(f64(vs))[:, :1, :]
    y = mxq(w, 2, "e4m3") @ mxq(pick(v).transpose(0, 2, 1), 1, "e4m3")
    y = y / total
    return y

@@ -1,0 +1,189 @@
+from contextlib import ExitStack
+
+import concourse.mybir as mybir
+from concourse.masks import make_identity
+
+D, NQ, N, T, DV = 512, 256, 512, 1024, 128
+FLOPS = 2 * NQ * N * D + 2 * NQ * N * DV
+
+F32 = mybir.dt.float32
+BF16 = mybir.dt.bfloat16
+I32 = mybir.dt.int32
+U32 = mybir.dt.uint32
+U16 = mybir.dt.uint16
+U8 = mybir.dt.uint8
+FP8X4 = mybir.dt.float8_e4m3fn_x4
+ALU = mybir.AluOpType
+ACT = mybir.ActivationFunctionType
+AX = mybir.AxisListType
+
+P = 128
+PACK = 4
+RUN = 8
+QB = NQ // P
+
+
+def tile_attend_soft_kb_srtq256n512t1024_kernel(tc, qT, k_words, k_scales, vT, vs, kb, offs, out):
+    nc = tc.nc
+    with ExitStack() as ctx:
+        sb = ctx.enter_context(tc.tile_pool(name="sb", bufs=1))
+        ps = ctx.enter_context(tc.psum_pool(name="ps", bufs=1))
+
+        def sbuf(name, shape, dtype):
+            return sb.tile(shape, dtype, name=name, align_bytes=64)
+
+        def turned(ap):
+            return ap.rearrange("p t (b r) -> p b t r", r=RUN)
+
+        offsets = sb.tile([P, N // 16], U16, name="offsets")
+        q_raw = sbuf("q_raw", [P, PACK, NQ], F32)
+        kw_pool = sbuf("kw_pool", [P, T], I32)
+        ks_pool = sbuf("ks_pool", [P, T // 4], I32)
+        kb_pool = sbuf("kb_pool", [P, T], F32)
+        v_pool = sbuf("v_pool", [P, T], F32)
+        vs_pool = sbuf("vs_pool", [P, T], F32)
+
+        nc.vector.memset(ks_pool[:], 0)
+        nc.vector.memset(vs_pool[:], 0.0)
+
+        nc.sync.dma_start(offsets[:], offs)
+        nc.sync.dma_start(q_raw[:], qT[0].rearrange("(p j) q -> p j q", j=PACK))
+        nc.sync.dma_start(kw_pool[:], k_words[0].rearrange("p n t -> p (n t)").bitcast(I32))
+        for quad in range(4):
+            nc.scalar.dma_start(ks_pool[32 * quad : 32 * quad + 4, :], k_scales[0, 4 * quad : 4 * quad + 4, :].bitcast(I32))
+        nc.scalar.dma_start(vs_pool[0:1, :], vs[0:1, :])
+        nc.sync.dma_start(kb_pool[:], kb)
+        nc.sync.dma_start(v_pool[:], vT)
+
+        ident = sbuf("ident", [P, P], F32)
+        make_identity(nc, ident[:])
+        ident_bf = sbuf("ident_bf", [P, P], BF16)
+        make_identity(nc, ident_bf[:])
+
+        warm = sbuf("warm", [P, 1], F32)
+        nc.scalar.activation(warm[:], ident[:, 0:1], ACT.Exp)
+
+        ks_g = sbuf("ks_g", [P, N], U8)
+        nc.vector.tensor_copy(ks_g[:], ks_pool[:].bitcast(U8).indirect(offsets[:]))
+        vs_list = sbuf("vs_list", [P, N], F32)
+        nc.vector.tensor_copy(vs_list[:], vs_pool[:].indirect(offsets[:]))
+
+        q_bf = sbuf("q_bf", [P, NQ, PACK], BF16)
+        q_codes = sbuf("q_codes", [P, NQ], U32)
+        q_scales = sbuf("q_scales", [P, NQ], U8)
+        kw_g = sbuf("kw_g", [P, N], U32)
+        kb_g = sbuf("kb_g", [P, N], F32)
+
+        def cols(b):
+            return slice(b * P, (b + 1) * P)
+
+        def quantise_queries(b):
+            nc.vector.quantize_mx(
+                out=q_codes[:, cols(b)].bitcast(FP8X4),
+                scales=q_scales[:, cols(b)],
+                in_=q_bf[:, cols(b), :].rearrange("p q j -> p (q j)"),
+            )
+
+        for b in range(QB):
+            nc.scalar.copy(q_bf[:, cols(b), :], q_raw[:, :, cols(b)].rearrange("p j q -> p q j"))
+        quantise_queries(0)
+        nc.vector.tensor_copy(kw_g[:], kw_pool[:].bitcast(U32).indirect(offsets[:]))
+        quantise_queries(1)
+        nc.vector.tensor_copy(kb_g[:], kb_pool[:].indirect(offsets[:]))
+
+        vs_g = sbuf("vs_g", [P, PACK, P], F32)
+        nc.scalar.copy(turned(vs_g[:]), vs_list[:].rearrange("p (b t r) -> p b t r", t=PACK, r=RUN))
+        vs_ps = ps.tile([P, PACK, P], F32, name="vs_ps")
+        for t in range(PACK):
+            nc.tensor.transpose(vs_ps[:, t, :], vs_g[:, t, :], ident[:])
+        vs_col = sbuf("vs_col", [P, PACK], F32)
+        nc.scalar.copy(vs_col[:], vs_ps[:, :, 0])
+
+        score_ps = [ps.tile([P, N], F32, name=f"score_ps{b}") for b in range(QB)]
+        for b in range(QB):
+            nc.tensor.matmul_mx(
+                out=score_ps[b][:],
+                lhsT=q_codes[:, cols(b)].bitcast(FP8X4),
+                lhsT_scale=q_scales[:, cols(b)],
+                rhs=kw_g[:].bitcast(FP8X4),
+                rhs_scale=ks_g[:],
+                start=True,
+                stop=True,
+            )
+
+        v_bf = sbuf("v_bf", [P, T], BF16)
+        nc.scalar.copy(v_bf[:], v_pool[:])
+        v_g = sbuf("v_g", [P, PACK, P], BF16)
+        nc.scalar.activation(turned(v_g[:]), v_bf[:].indirect(offsets[:]), ACT.Copy)
+        v_ps = ps.tile([P, PACK, P], BF16, name="v_ps")
+        for t in range(PACK):
+            nc.tensor.transpose(v_ps[:, t, :], v_g[:, t, :], ident_bf[:])
+
+        s = [sbuf(f"s{b}", [P, N], F32) for b in range(QB)]
+        neg_max = [sbuf(f"neg_max{b}", [P, 1], F32) for b in range(QB)]
+        for b in range(QB):
+            nc.vector.tensor_tensor(s[b][:], score_ps[b][:], kb_g[:], ALU.add)
+        for b in range(QB):
+            nc.vector.tensor_reduce(neg_max[b][:], s[b][:], AX.X, ALU.max, negate=True)
+
+        p = [sbuf(f"p{b}", [P, PACK, P], F32) for b in range(QB)]
+        row_sum = [sbuf(f"row_sum{b}", [P, 1], F32) for b in range(QB)]
+        p_ps = [ps.tile([P, PACK, P], F32, name=f"p_ps{b}") for b in range(QB)]
+        for b in range(QB):
+            nc.scalar.activation(
+                p[b][:].rearrange("p t (b r) -> p t b r", r=RUN),
+                s[b][:].rearrange("p (b t r) -> p t b r", t=PACK, r=RUN),
+                ACT.Exp,
+                bias=neg_max[b][:],
+                accum_out=row_sum[b][:],
+            )
+            for t in range(PACK):
+                nc.tensor.transpose(p_ps[b][:, t, :], p[b][:, t, :], ident[:])
+
+        v_k = sbuf("v_k", [P, DV, PACK], BF16)
+        nc.scalar.copy(v_k[:], v_ps[:].rearrange("p t e -> p e t"))
+
+        w = [sbuf(f"w{b}", [P, P, PACK], BF16) for b in range(QB)]
+        w_codes = [sbuf(f"w_codes{b}", [P, P], U32) for b in range(QB)]
+        w_scales = [sbuf(f"w_scales{b}", [P, P], U8) for b in range(QB)]
+        v_codes = sbuf("v_codes", [P, DV], U32)
+        v_scales = sbuf("v_scales", [P, DV], U8)
+        inv_sum = [sbuf(f"inv_sum{b}", [P, 1], F32) for b in range(QB)]
+
+        def weigh(b):
+            nc.vector.tensor_tensor(
+                w[b][:],
+                p_ps[b][:].rearrange("p t q -> p q t"),
+                vs_col[:].unsqueeze(1).to_broadcast([P, P, PACK]),
+                ALU.mult,
+            )
+
+        def quantise_weights(b):
+            nc.vector.quantize_mx(
+                out=w_codes[b][:].bitcast(FP8X4), scales=w_scales[b][:], in_=w[b][:].rearrange("p q t -> p (q t)")
+            )
+
+        nc.vector.reciprocal(inv_sum[0][:], row_sum[0][:])
+        weigh(0)
+        nc.vector.reciprocal(inv_sum[1][:], row_sum[1][:])
+        nc.vector.quantize_mx(
+            out=v_codes[:].bitcast(FP8X4), scales=v_scales[:], in_=v_k[:].rearrange("p e t -> p (e t)")
+        )
+        quantise_weights(0)
+        weigh(1)
+        quantise_weights(1)
+
+        for b in range(QB):
+            y_ps = ps.tile([P, DV], F32, name=f"y_ps{b}")
+            nc.tensor.matmul_mx(
+                out=y_ps[:],
+                lhsT=w_codes[b][:].bitcast(FP8X4),
+                lhsT_scale=w_scales[b][:],
+                rhs=v_codes[:].bitcast(FP8X4),
+                rhs_scale=v_scales[:],
+                start=True,
+                stop=True,
+            )
+            y = sbuf(f"y{b}", [P, DV], F32)
+            nc.scalar.activation(y[:], y_ps[:], ACT.Copy, scale=inv_sum[b][:])
+            nc.sync.dma_start(out[0, cols(b), :], y[:])

@@ -29,8 +29,8 @@ def tile_attend_soft_kb_srtq256n512t1024_kernel(tc, qT, k_words, k_scales, vT, v
         sb = ctx.enter_context(tc.tile_pool(name="sb", bufs=1))
         ps = ctx.enter_context(tc.psum_pool(name="ps", bufs=1))
 
-        def sbuf(name, shape, dtype):
-            return sb.tile(shape, dtype, name=name, align_bytes=64)
+        def sbuf(name, shape, dtype, tag=None):
+            return sb.tile(shape, dtype, name=name, tag=tag or name, align_bytes=64)
 
         def turned(ap):
             return ap.rearrange("p t (b r) -> p b t r", r=RUN)
@@ -43,15 +43,19 @@ def tile_attend_soft_kb_srtq256n512t1024_kernel(tc, qT, k_words, k_scales, vT, v
         v_pool = sbuf("v_pool", [P, T], F32)
         vs_pool = sbuf("vs_pool", [P, T], F32)
 
-        nc.vector.memset(ks_pool[:], 0)
-        nc.vector.memset(vs_pool[:], 0.0)
+        warm = sbuf("warm", [P, 1], F32)
+        nc.gpsimd.memset(ks_pool[:], 0)
+        nc.gpsimd.memset(vs_pool[:, :448], 0.0)
+        nc.vector.memset(vs_pool[:, 448:], 0.0)
+        nc.vector.memset(warm[:], 0.0)
 
         nc.sync.dma_start(offsets[:], offs)
+        for quad in range(4):
+            queue = nc.sync if quad < 2 else nc.scalar
+            queue.dma_start(ks_pool[32 * quad : 32 * quad + 4, :], k_scales[0, 4 * quad : 4 * quad + 4, :].bitcast(I32))
+        nc.scalar.dma_start(vs_pool[0:1, :], vs[0:1, :])
         nc.sync.dma_start(q_raw[:], qT[0].rearrange("(p j) q -> p j q", j=PACK))
         nc.sync.dma_start(kw_pool[:], k_words[0].rearrange("p n t -> p (n t)").bitcast(I32))
-        for quad in range(4):
-            nc.scalar.dma_start(ks_pool[32 * quad : 32 * quad + 4, :], k_scales[0, 4 * quad : 4 * quad + 4, :].bitcast(I32))
-        nc.scalar.dma_start(vs_pool[0:1, :], vs[0:1, :])
         nc.sync.dma_start(kb_pool[:], kb)
         nc.sync.dma_start(v_pool[:], vT)
 
@@ -60,8 +64,7 @@ def tile_attend_soft_kb_srtq256n512t1024_kernel(tc, qT, k_words, k_scales, vT, v
         ident_bf = sbuf("ident_bf", [P, P], BF16)
         make_identity(nc, ident_bf[:])
 
-        warm = sbuf("warm", [P, 1], F32)
-        nc.scalar.activation(warm[:], ident[:, 0:1], ACT.Exp)
+        nc.scalar.activation(warm[:], warm[:], ACT.Exp)
 
         ks_g = sbuf("ks_g", [P, N], U8)
         nc.vector.tensor_copy(ks_g[:], ks_pool[:].bitcast(U8).indirect(offsets[:]))
@@ -93,11 +96,6 @@ def tile_attend_soft_kb_srtq256n512t1024_kernel(tc, qT, k_words, k_scales, vT, v
 
         vs_g = sbuf("vs_g", [P, PACK, P], F32)
         nc.scalar.copy(turned(vs_g[:]), vs_list[:].rearrange("p (b t r) -> p b t r", t=PACK, r=RUN))
-        vs_ps = ps.tile([P, PACK, P], F32, name="vs_ps")
-        for t in range(PACK):
-            nc.tensor.transpose(vs_ps[:, t, :], vs_g[:, t, :], ident[:])
-        vs_col = sbuf("vs_col", [P, PACK], F32)
-        nc.scalar.copy(vs_col[:], vs_ps[:, :, 0])
 
         score_ps = [ps.tile([P, N], F32, name=f"score_ps{b}") for b in range(QB)]
         for b in range(QB):
@@ -111,7 +109,13 @@ def tile_attend_soft_kb_srtq256n512t1024_kernel(tc, qT, k_words, k_scales, vT, v
                 stop=True,
             )
 
-        v_bf = sbuf("v_bf", [P, T], BF16)
+        vs_ps = ps.tile([P, PACK, P], F32, name="vs_ps")
+        for t in range(PACK):
+            nc.tensor.transpose(vs_ps[:, t, :], vs_g[:, t, :], ident[:])
+        vs_col = sbuf("vs_col", [P, PACK], F32)
+        nc.scalar.copy(vs_col[:], vs_ps[:, :, 0])
+
+        v_bf = sbuf("v_bf", [P, T], BF16, tag="v_bf_then_p0")
         nc.scalar.copy(v_bf[:], v_pool[:])
         v_g = sbuf("v_g", [P, PACK, P], BF16)
         nc.scalar.activation(turned(v_g[:]), v_bf[:].indirect(offsets[:]), ACT.Copy)
@@ -126,7 +130,7 @@ def tile_attend_soft_kb_srtq256n512t1024_kernel(tc, qT, k_words, k_scales, vT, v
         for b in range(QB):
             nc.vector.tensor_reduce(neg_max[b][:], s[b][:], AX.X, ALU.max, negate=True)
 
-        p = [sbuf(f"p{b}", [P, PACK, P], F32) for b in range(QB)]
+        p = [sbuf("p0", [P, PACK, P], F32, tag="v_bf_then_p0"), sbuf("p1", [P, PACK, P], F32)]
         row_sum = [sbuf(f"row_sum{b}", [P, 1], F32) for b in range(QB)]
         p_ps = [ps.tile([P, PACK, P], F32, name=f"p_ps{b}") for b in range(QB)]
         for b in range(QB):
@@ -163,14 +167,14 @@ def tile_attend_soft_kb_srtq256n512t1024_kernel(tc, qT, k_words, k_scales, vT, v
                 out=w_codes[b][:].bitcast(FP8X4), scales=w_scales[b][:], in_=w[b][:].rearrange("p q t -> p (q t)")
             )
 
-        nc.vector.reciprocal(inv_sum[0][:], row_sum[0][:])
         weigh(0)
-        nc.vector.reciprocal(inv_sum[1][:], row_sum[1][:])
         nc.vector.quantize_mx(
             out=v_codes[:].bitcast(FP8X4), scales=v_scales[:], in_=v_k[:].rearrange("p e t -> p (e t)")
         )
-        quantise_weights(0)
+        nc.vector.reciprocal(inv_sum[0][:], row_sum[0][:])
+        nc.vector.reciprocal(inv_sum[1][:], row_sum[1][:])
         weigh(1)
+        quantise_weights(0)
         quantise_weights(1)
 
         for b in range(QB):
@@ -185,5 +189,8 @@ def tile_attend_soft_kb_srtq256n512t1024_kernel(tc, qT, k_words, k_scales, vT, v
                 stop=True,
             )
             y = sbuf(f"y{b}", [P, DV], F32)
-            nc.scalar.activation(y[:], y_ps[:], ACT.Copy, scale=inv_sum[b][:])
+            if b == 0:
+                nc.scalar.activation(y[:], y_ps[:], ACT.Copy, scale=inv_sum[b][:])
+            else:
+                nc.vector.tensor_scalar(y[:], y_ps[:], inv_sum[b][:], None, ALU.mult)
             nc.sync.dma_start(out[0, cols(b), :], y[:])

@@ -35,36 +35,36 @@ def tile_attend_soft_kb_srtq256n512t1024_kernel(tc, qT, k_words, k_scales, vT, v
         def turned(ap):
             return ap.rearrange("p t (b r) -> p b t r", r=RUN)
 
+        halves = [slice(0, T // 2), slice(T // 2, T)]
         offsets = sb.tile([P, N // 16], U16, name="offsets")
         q_raw = sbuf("q_raw", [P, PACK, NQ], F32)
-        kw_pool = sbuf("kw_pool", [P, T], I32)
+        kw_pool = sbuf("kw_pool", [P, T], I32, tag="kw_pool_then_q_codes1")
         ks_pool = sbuf("ks_pool", [P, T // 4], I32)
         kb_pool = sbuf("kb_pool", [P, T], F32)
         v_pool = sbuf("v_pool", [P, T], F32)
-        vs_pool = sbuf("vs_pool", [P, T], F32)
+        vs_pool = sbuf("vs_pool", [P, T], F32, tag="vs_pool_then_q_codes0")
 
         warm = sbuf("warm", [P, 1], F32)
-        nc.gpsimd.memset(ks_pool[:], 0)
-        nc.gpsimd.memset(vs_pool[:, :448], 0.0)
-        nc.vector.memset(vs_pool[:, 448:], 0.0)
-        nc.vector.memset(warm[:], 0.0)
+        nc.vector.memset(ks_pool[:], 0)
+        nc.vector.memset(vs_pool[:], 0.0)
 
         nc.sync.dma_start(offsets[:], offs)
         for quad in range(4):
             queue = nc.sync if quad < 2 else nc.scalar
             queue.dma_start(ks_pool[32 * quad : 32 * quad + 4, :], k_scales[0, 4 * quad : 4 * quad + 4, :].bitcast(I32))
-        nc.scalar.dma_start(vs_pool[0:1, :], vs[0:1, :])
         nc.sync.dma_start(q_raw[:], qT[0].rearrange("(p j) q -> p j q", j=PACK))
+        nc.sync.dma_start(vs_pool[0:1, :], vs[0:1, :])
         nc.sync.dma_start(kw_pool[:], k_words[0].rearrange("p n t -> p (n t)").bitcast(I32))
         nc.sync.dma_start(kb_pool[:], kb)
-        nc.sync.dma_start(v_pool[:], vT)
+        for half in halves:
+            nc.sync.dma_start(v_pool[:, half], vT[:, half])
 
         ident = sbuf("ident", [P, P], F32)
         make_identity(nc, ident[:])
         ident_bf = sbuf("ident_bf", [P, P], BF16)
         make_identity(nc, ident_bf[:])
 
-        nc.scalar.activation(warm[:], warm[:], ACT.Exp)
+        nc.scalar.activation(warm[:], q_raw[:, 0, 0:1], ACT.Exp, scale=0.0)
 
         ks_g = sbuf("ks_g", [P, N], U8)
         nc.vector.tensor_copy(ks_g[:], ks_pool[:].bitcast(U8).indirect(offsets[:]))
@@ -72,7 +72,10 @@ def tile_attend_soft_kb_srtq256n512t1024_kernel(tc, qT, k_words, k_scales, vT, v
         nc.vector.tensor_copy(vs_list[:], vs_pool[:].indirect(offsets[:]))
 
         q_bf = sbuf("q_bf", [P, NQ, PACK], BF16)
-        q_codes = sbuf("q_codes", [P, NQ], U32)
+        q_codes = [
+            sbuf("q_codes0", [P, P], U32, tag="vs_pool_then_q_codes0"),
+            sbuf("q_codes1", [P, P], U32, tag="kw_pool_then_q_codes1"),
+        ]
         q_scales = sbuf("q_scales", [P, NQ], U8)
         kw_g = sbuf("kw_g", [P, N], U32)
         kb_g = sbuf("kb_g", [P, N], F32)
@@ -82,7 +85,7 @@ def tile_attend_soft_kb_srtq256n512t1024_kernel(tc, qT, k_words, k_scales, vT, v
 
         def quantise_queries(b):
             nc.vector.quantize_mx(
-                out=q_codes[:, cols(b)].bitcast(FP8X4),
+                out=q_codes[b][:].bitcast(FP8X4),
                 scales=q_scales[:, cols(b)],
                 in_=q_bf[:, cols(b), :].rearrange("p q j -> p (q j)"),
             )
@@ -101,7 +104,7 @@ def tile_attend_soft_kb_srtq256n512t1024_kernel(tc, qT, k_words, k_scales, vT, v
         for b in range(QB):
             nc.tensor.matmul_mx(
                 out=score_ps[b][:],
-                lhsT=q_codes[:, cols(b)].bitcast(FP8X4),
+                lhsT=q_codes[b][:].bitcast(FP8X4),
                 lhsT_scale=q_scales[:, cols(b)],
                 rhs=kw_g[:].bitcast(FP8X4),
                 rhs_scale=ks_g[:],
@@ -116,7 +119,8 @@ def tile_attend_soft_kb_srtq256n512t1024_kernel(tc, qT, k_words, k_scales, vT, v
         nc.scalar.copy(vs_col[:], vs_ps[:, :, 0])
 
         v_bf = sbuf("v_bf", [P, T], BF16, tag="v_bf_then_p0")
-        nc.scalar.copy(v_bf[:], v_pool[:])
+        for half in halves:
+            nc.scalar.copy(v_bf[:, half], v_pool[:, half])
         v_g = sbuf("v_g", [P, PACK, P], BF16)
         nc.scalar.activation(turned(v_g[:]), v_bf[:].indirect(offsets[:]), ACT.Copy)
         v_ps = ps.tile([P, PACK, P], BF16, name="v_ps")

@@ -27,6 +27,7 @@ def tile_attend_soft_kb_srtq256n512t1024_kernel(tc, qT, k_words, k_scales, vT, v
     nc = tc.nc
     with ExitStack() as ctx:
         sb = ctx.enter_context(tc.tile_pool(name="sb", bufs=1))
+        reuse = ctx.enter_context(tc.tile_pool(name="reuse", bufs=1))
         ps = ctx.enter_context(tc.psum_pool(name="ps", bufs=1))
 
         def sbuf(name, shape, dtype, tag=None):
@@ -38,11 +39,11 @@ def tile_attend_soft_kb_srtq256n512t1024_kernel(tc, qT, k_words, k_scales, vT, v
         halves = [slice(0, T // 2), slice(T // 2, T)]
         offsets = sb.tile([P, N // 16], U16, name="offsets")
         q_raw = sbuf("q_raw", [P, PACK, NQ], F32)
-        kw_pool = sbuf("kw_pool", [P, T], I32, tag="kw_pool_then_q_codes1")
+        kw_pool = sbuf("kw_pool", [P, T], I32)
         ks_pool = sbuf("ks_pool", [P, T // 4], I32)
         kb_pool = sbuf("kb_pool", [P, T], F32)
         v_pool = sbuf("v_pool", [P, T], F32)
-        vs_pool = sbuf("vs_pool", [P, T], F32, tag="vs_pool_then_q_codes0")
+        vs_pool = reuse.tile([P, T], F32, name="vs_pool", align_bytes=64, offset=0)
 
         warm = sbuf("warm", [P, 1], F32)
         nc.vector.memset(ks_pool[:], 0)
@@ -71,14 +72,17 @@ def tile_attend_soft_kb_srtq256n512t1024_kernel(tc, qT, k_words, k_scales, vT, v
         vs_list = sbuf("vs_list", [P, N], F32)
         nc.vector.tensor_copy(vs_list[:], vs_pool[:].indirect(offsets[:]))
 
-        q_bf = sbuf("q_bf", [P, NQ, PACK], BF16)
+        q_bf = [
+            sbuf("q_bf0", [P, P, PACK], BF16),
+            reuse.tile([P, P, PACK], BF16, name="q_bf1", align_bytes=64, offset=1024),
+        ]
         q_codes = [
-            sbuf("q_codes0", [P, P], U32, tag="vs_pool_then_q_codes0"),
-            sbuf("q_codes1", [P, P], U32, tag="kw_pool_then_q_codes1"),
+            reuse.tile([P, P], U32, name="q_codes0", align_bytes=64, offset=0),
+            sbuf("q_codes1", [P, P], U32),
         ]
         q_scales = sbuf("q_scales", [P, NQ], U8)
         kw_g = sbuf("kw_g", [P, N], U32)
-        kb_g = sbuf("kb_g", [P, N], F32)
+        kb_g = sbuf("kb_g", [P, N], F32, tag="kb_g_then_vs_col")
 
         def cols(b):
             return slice(b * P, (b + 1) * P)
@@ -87,11 +91,11 @@ def tile_attend_soft_kb_srtq256n512t1024_kernel(tc, qT, k_words, k_scales, vT, v
             nc.vector.quantize_mx(
                 out=q_codes[b][:].bitcast(FP8X4),
                 scales=q_scales[:, cols(b)],
-                in_=q_bf[:, cols(b), :].rearrange("p q j -> p (q j)"),
+                in_=q_bf[b][:].rearrange("p q j -> p (q j)"),
             )
 
         for b in range(QB):
-            nc.scalar.copy(q_bf[:, cols(b), :], q_raw[:, :, cols(b)].rearrange("p j q -> p q j"))
+            nc.scalar.copy(q_bf[b][:], q_raw[:, :, cols(b)].rearrange("p j q -> p q j"))
         quantise_queries(0)
         nc.vector.tensor_copy(kw_g[:], kw_pool[:].bitcast(U32).indirect(offsets[:]))
         quantise_queries(1)
@@ -115,8 +119,6 @@ def tile_attend_soft_kb_srtq256n512t1024_kernel(tc, qT, k_words, k_scales, vT, v
         vs_ps = ps.tile([P, PACK, P], F32, name="vs_ps")
         for t in range(PACK):
             nc.tensor.transpose(vs_ps[:, t, :], vs_g[:, t, :], ident[:])
-        vs_col = sbuf("vs_col", [P, PACK], F32)
-        nc.scalar.copy(vs_col[:], vs_ps[:, :, 0])
 
         v_bf = sbuf("v_bf", [P, T], BF16, tag="v_bf_then_p0")
         for half in halves:
@@ -133,18 +135,22 @@ def tile_attend_soft_kb_srtq256n512t1024_kernel(tc, qT, k_words, k_scales, vT, v
             nc.vector.tensor_tensor(s[b][:], score_ps[b][:], kb_g[:], ALU.add)
         for b in range(QB):
             nc.vector.tensor_reduce(neg_max[b][:], s[b][:], AX.X, ALU.max, negate=True)
+        vs_col = sbuf("vs_col", [P, PACK], F32, tag="kb_g_then_vs_col")
+        nc.vector.tensor_copy(vs_col[:], vs_ps[:, :, 0])
 
         p = [sbuf("p0", [P, PACK, P], F32, tag="v_bf_then_p0"), sbuf("p1", [P, PACK, P], F32)]
-        row_sum = [sbuf(f"row_sum{b}", [P, 1], F32) for b in range(QB)]
+        part_sum = sbuf("part_sum", [P, QB, 2], F32)
         p_ps = [ps.tile([P, PACK, P], F32, name=f"p_ps{b}") for b in range(QB)]
         for b in range(QB):
-            nc.scalar.activation(
-                p[b][:].rearrange("p t (b r) -> p t b r", r=RUN),
-                s[b][:].rearrange("p (b t r) -> p t b r", t=PACK, r=RUN),
-                ACT.Exp,
-                bias=neg_max[b][:],
-                accum_out=row_sum[b][:],
-            )
+            for h in range(2):
+                places = slice(2 * h, 2 * h + 2)
+                nc.scalar.activation(
+                    p[b][:, places, :].rearrange("p t (b r) -> p t b r", r=RUN),
+                    s[b][:].rearrange("p (b t r) -> p t b r", t=PACK, r=RUN)[:, places],
+                    ACT.Exp,
+                    bias=neg_max[b][:],
+                    accum_out=part_sum[:, b, h : h + 1],
+                )
             for t in range(PACK):
                 nc.tensor.transpose(p_ps[b][:, t, :], p[b][:, t, :], ident[:])
 
@@ -156,7 +162,8 @@ def tile_attend_soft_kb_srtq256n512t1024_kernel(tc, qT, k_words, k_scales, vT, v
         w_scales = [sbuf(f"w_scales{b}", [P, P], U8) for b in range(QB)]
         v_codes = sbuf("v_codes", [P, DV], U32)
         v_scales = sbuf("v_scales", [P, DV], U8)
-        inv_sum = [sbuf(f"inv_sum{b}", [P, 1], F32) for b in range(QB)]
+        row_sum = sbuf("row_sum", [P, QB], F32)
+        inv_sum = sbuf("inv_sum", [P, QB], F32)
 
         def weigh(b):
             nc.vector.tensor_tensor(
@@ -171,12 +178,12 @@ def tile_attend_soft_kb_srtq256n512t1024_kernel(tc, qT, k_words, k_scales, vT, v
                 out=w_codes[b][:].bitcast(FP8X4), scales=w_scales[b][:], in_=w[b][:].rearrange("p q t -> p (q t)")
             )
 
+        nc.vector.tensor_reduce(row_sum[:], part_sum[:], AX.X, ALU.add)
+        nc.vector.reciprocal(inv_sum[:], row_sum[:])
         weigh(0)
         nc.vector.quantize_mx(
             out=v_codes[:].bitcast(FP8X4), scales=v_scales[:], in_=v_k[:].rearrange("p e t -> p (e t)")
         )
-        nc.vector.reciprocal(inv_sum[0][:], row_sum[0][:])
-        nc.vector.reciprocal(inv_sum[1][:], row_sum[1][:])
         weigh(1)
         quantise_weights(0)
         quantise_weights(1)
@@ -194,7 +201,7 @@ def tile_attend_soft_kb_srtq256n512t1024_kernel(tc, qT, k_words, k_scales, vT, v
             )
             y = sbuf(f"y{b}", [P, DV], F32)
             if b == 0:
-                nc.scalar.activation(y[:], y_ps[:], ACT.Copy, scale=inv_sum[b][:])
+                nc.scalar.activation(y[:], y_ps[:], ACT.Copy, scale=inv_sum[:, b : b + 1])
             else:
-                nc.vector.tensor_scalar(y[:], y_ps[:], inv_sum[b][:], None, ALU.mult)
+                nc.vector.tensor_scalar(y[:], y_ps[:], inv_sum[:, b : b + 1], None, ALU.mult)
             nc.sync.dma_start(out[0, cols(b), :], y[:])

@@ -19,7 +19,6 @@ AX = mybir.AxisListType
 
 P = 128
 PACK = 4
-RUN = 8
 QB = NQ // P
 
 
@@ -33,21 +32,27 @@ def tile_attend_soft_kb_srtq256n512t1024_kernel(tc, qT, k_words, k_scales, vT, v
         def sbuf(name, shape, dtype, tag=None):
             return sb.tile(shape, dtype, name=name, tag=tag or name, align_bytes=64)
 
-        def turned(ap):
-            return ap.rearrange("p t (b r) -> p b t r", r=RUN)
+        def shared(name, shape, dtype, offset):
+            return reuse.tile(shape, dtype, name=name, align_bytes=64, offset=offset)
+
+        def cols(b):
+            return slice(b * P, (b + 1) * P)
 
         halves = [slice(0, T // 2), slice(T // 2, T)]
         offsets = sb.tile([P, N // 16], U16, name="offsets")
-        q_raw = sbuf("q_raw", [P, PACK, NQ], F32)
+        q_raw = shared("q_raw", [P, PACK, NQ], F32, 0)
         kw_pool = sbuf("kw_pool", [P, T], I32)
         ks_pool = sbuf("ks_pool", [P, T // 4], I32)
         kb_pool = sbuf("kb_pool", [P, T], F32)
         v_pool = sbuf("v_pool", [P, T], F32)
-        vs_pool = reuse.tile([P, T], F32, name="vs_pool", align_bytes=64, offset=0)
+        vs_pool = sbuf("vs_pool", [P, T], F32)
+        ident = sbuf("ident", [P, P], F32)
 
         warm = sbuf("warm", [P, 1], F32)
         nc.vector.memset(ks_pool[:], 0)
-        nc.vector.memset(vs_pool[:], 0.0)
+        nc.vector.memset(vs_pool[:].bitcast(I32), 0)
+        nc.vector.memset(ident[:], 0.0)
+        make_identity(nc, ident[:], nomemset=True)
 
         nc.sync.dma_start(offsets[:], offs)
         for quad in range(4):
@@ -60,32 +65,18 @@ def tile_attend_soft_kb_srtq256n512t1024_kernel(tc, qT, k_words, k_scales, vT, v
         for half in halves:
             nc.sync.dma_start(v_pool[:, half], vT[:, half])
 
-        ident = sbuf("ident", [P, P], F32)
-        make_identity(nc, ident[:])
-        ident_bf = sbuf("ident_bf", [P, P], BF16)
-        make_identity(nc, ident_bf[:])
-
         nc.scalar.activation(warm[:], q_raw[:, 0, 0:1], ACT.Exp, scale=0.0)
 
         ks_g = sbuf("ks_g", [P, N], U8)
         nc.vector.tensor_copy(ks_g[:], ks_pool[:].bitcast(U8).indirect(offsets[:]))
-        vs_list = sbuf("vs_list", [P, N], F32)
-        nc.vector.tensor_copy(vs_list[:], vs_pool[:].indirect(offsets[:]))
+        vs_g = sbuf("vs_g", [P, N], F32)
+        nc.vector.tensor_copy(vs_g[:], vs_pool[:].indirect(offsets[:]))
 
-        q_bf = [
-            sbuf("q_bf0", [P, P, PACK], BF16),
-            reuse.tile([P, P, PACK], BF16, name="q_bf1", align_bytes=64, offset=1024),
-        ]
-        q_codes = [
-            reuse.tile([P, P], U32, name="q_codes0", align_bytes=64, offset=0),
-            sbuf("q_codes1", [P, P], U32),
-        ]
+        q_bf = [sbuf(f"q_bf{b}", [P, P, PACK], BF16) for b in range(QB)]
+        q_codes = [sbuf("q_codes0", [P, P], U32), shared("q_codes1", [P, P], U32, 4096)]
         q_scales = sbuf("q_scales", [P, NQ], U8)
         kw_g = sbuf("kw_g", [P, N], U32)
-        kb_g = sbuf("kb_g", [P, N], F32, tag="kb_g_then_vs_col")
-
-        def cols(b):
-            return slice(b * P, (b + 1) * P)
+        kb_g = shared("kb_g", [P, N], F32, 0)
 
         def quantise_queries(b):
             nc.vector.quantize_mx(
@@ -101,9 +92,6 @@ def tile_attend_soft_kb_srtq256n512t1024_kernel(tc, qT, k_words, k_scales, vT, v
         quantise_queries(1)
         nc.vector.tensor_copy(kb_g[:], kb_pool[:].indirect(offsets[:]))
 
-        vs_g = sbuf("vs_g", [P, PACK, P], F32)
-        nc.scalar.copy(turned(vs_g[:]), vs_list[:].rearrange("p (b t r) -> p b t r", t=PACK, r=RUN))
-
         score_ps = [ps.tile([P, N], F32, name=f"score_ps{b}") for b in range(QB)]
         for b in range(QB):
             nc.tensor.matmul_mx(
@@ -118,25 +106,33 @@ def tile_attend_soft_kb_srtq256n512t1024_kernel(tc, qT, k_words, k_scales, vT, v
 
         vs_ps = ps.tile([P, PACK, P], F32, name="vs_ps")
         for t in range(PACK):
-            nc.tensor.transpose(vs_ps[:, t, :], vs_g[:, t, :], ident[:])
+            nc.tensor.transpose(vs_ps[:, t, :], vs_g[:, t:N:PACK], ident[:])
 
         v_bf = sbuf("v_bf", [P, T], BF16, tag="v_bf_then_p0")
         for half in halves:
             nc.scalar.copy(v_bf[:, half], v_pool[:, half])
-        v_g = sbuf("v_g", [P, PACK, P], BF16)
-        nc.scalar.activation(turned(v_g[:]), v_bf[:].indirect(offsets[:]), ACT.Copy)
-        v_ps = ps.tile([P, PACK, P], BF16, name="v_ps")
-        for t in range(PACK):
-            nc.tensor.transpose(v_ps[:, t, :], v_g[:, t, :], ident_bf[:])
+        v_g = sbuf("v_g", [P, N], BF16)
+        nc.scalar.activation(v_g[:], v_bf[:].indirect(offsets[:]), ACT.Copy)
+        v_ps = ps.tile([P, 2, P], F32, name="v_ps")
+        v_words = v_g[:].bitcast(F32)
+        for u in range(2):
+            nc.tensor.transpose(v_ps[:, u, :], v_words[:, u : N // 2 : 2], ident[:])
 
         s = [sbuf(f"s{b}", [P, N], F32) for b in range(QB)]
-        neg_max = [sbuf(f"neg_max{b}", [P, 1], F32) for b in range(QB)]
+        neg_max = [shared("neg_max0", [P, 1], F32, 4096), sbuf("neg_max1", [P, 1], F32)]
         for b in range(QB):
             nc.vector.tensor_tensor(s[b][:], score_ps[b][:], kb_g[:], ALU.add)
         for b in range(QB):
             nc.vector.tensor_reduce(neg_max[b][:], s[b][:], AX.X, ALU.max, negate=True)
-        vs_col = sbuf("vs_col", [P, PACK], F32, tag="kb_g_then_vs_col")
+        vs_col = shared("vs_col", [P, PACK], F32, 0)
         nc.vector.tensor_copy(vs_col[:], vs_ps[:, :, 0])
+        v_k = shared("v_k", [P, DV, PACK], BF16, 64)
+        nc.vector.tensor_copy(v_k[:].bitcast(F32), v_ps[:].rearrange("p u e -> p e u"))
+        v_codes = sbuf("v_codes", [P, DV], U32)
+        v_scales = sbuf("v_scales", [P, DV], U8)
+        nc.vector.quantize_mx(
+            out=v_codes[:].bitcast(FP8X4), scales=v_scales[:], in_=v_k[:].rearrange("p e t -> p (e t)")
+        )
 
         p = [sbuf("p0", [P, PACK, P], F32, tag="v_bf_then_p0"), sbuf("p1", [P, PACK, P], F32)]
         part_sum = sbuf("part_sum", [P, QB, 2], F32)
@@ -145,8 +141,8 @@ def tile_attend_soft_kb_srtq256n512t1024_kernel(tc, qT, k_words, k_scales, vT, v
             for h in range(2):
                 places = slice(2 * h, 2 * h + 2)
                 nc.scalar.activation(
-                    p[b][:, places, :].rearrange("p t (b r) -> p t b r", r=RUN),
-                    s[b][:].rearrange("p (b t r) -> p t b r", t=PACK, r=RUN)[:, places],
+                    p[b][:, places, :].rearrange("p t s -> p s t"),
+                    s[b][:].rearrange("p (s t) -> p s t", t=PACK)[:, :, places],
                     ACT.Exp,
                     bias=neg_max[b][:],
                     accum_out=part_sum[:, b, h : h + 1],
@@ -154,14 +150,9 @@ def tile_attend_soft_kb_srtq256n512t1024_kernel(tc, qT, k_words, k_scales, vT, v
             for t in range(PACK):
                 nc.tensor.transpose(p_ps[b][:, t, :], p[b][:, t, :], ident[:])
 
-        v_k = sbuf("v_k", [P, DV, PACK], BF16)
-        nc.scalar.copy(v_k[:], v_ps[:].rearrange("p t e -> p e t"))
-
         w = [sbuf(f"w{b}", [P, P, PACK], BF16) for b in range(QB)]
         w_codes = [sbuf(f"w_codes{b}", [P, P], U32) for b in range(QB)]
         w_scales = [sbuf(f"w_scales{b}", [P, P], U8) for b in range(QB)]
-        v_codes = sbuf("v_codes", [P, DV], U32)
-        v_scales = sbuf("v_scales", [P, DV], U8)
         row_sum = sbuf("row_sum", [P, QB], F32)
         inv_sum = sbuf("inv_sum", [P, QB], F32)
 
@@ -178,15 +169,12 @@ def tile_attend_soft_kb_srtq256n512t1024_kernel(tc, qT, k_words, k_scales, vT, v
                 out=w_codes[b][:].bitcast(FP8X4), scales=w_scales[b][:], in_=w[b][:].rearrange("p q t -> p (q t)")
             )
 
-        nc.vector.tensor_reduce(row_sum[:], part_sum[:], AX.X, ALU.add)
-        nc.vector.reciprocal(inv_sum[:], row_sum[:])
         weigh(0)
-        nc.vector.quantize_mx(
-            out=v_codes[:].bitcast(FP8X4), scales=v_scales[:], in_=v_k[:].rearrange("p e t -> p (e t)")
-        )
         weigh(1)
         quantise_weights(0)
         quantise_weights(1)
+        nc.vector.tensor_reduce(row_sum[:], part_sum[:], AX.X, ALU.add)
+        nc.vector.reciprocal(inv_sum[:], row_sum[:])
 
         for b in range(QB):
             y_ps = ps.tile([P, DV], F32, name=f"y_ps{b}")

@@ -50,32 +50,34 @@ def tile_attend_soft_kb_srtq256n512t1024_kernel(tc, qT, k_words, k_scales, vT, v
 
         warm = sbuf("warm", [P, 1], F32)
         nc.vector.memset(ks_pool[:], 0)
-        nc.vector.memset(vs_pool[:].bitcast(I32), 0)
+        nc.vector.memset(vs_pool[0 : P - 1, :].bitcast(I32), 0)
         nc.vector.memset(ident[:], 0.0)
         make_identity(nc, ident[:], nomemset=True)
 
         nc.sync.dma_start(offsets[:], offs)
-        for quad in range(4):
-            queue = nc.sync if quad < 2 else nc.scalar
-            queue.dma_start(ks_pool[32 * quad : 32 * quad + 4, :], k_scales[0, 4 * quad : 4 * quad + 4, :].bitcast(I32))
-        nc.sync.dma_start(q_raw[:], qT[0].rearrange("(p j) q -> p j q", j=PACK))
-        nc.sync.dma_start(vs_pool[0:1, :], vs[0:1, :])
+        nc.sync.dma_start(vs_pool[P - 1 : P, :], vs[0:1, :])
         nc.sync.dma_start(kw_pool[:], k_words[0].rearrange("p n t -> p (n t)").bitcast(I32))
+        for quad in range(4):
+            nc.sync.dma_start(ks_pool[32 * quad : 32 * quad + 4, :], k_scales[0, 4 * quad : 4 * quad + 4, :].bitcast(I32))
+        nc.sync.dma_start(q_raw[:], qT[0].rearrange("(p j) q -> p j q", j=PACK))
         nc.sync.dma_start(kb_pool[:], kb)
         for half in halves:
             nc.sync.dma_start(v_pool[:, half], vT[:, half])
 
-        nc.scalar.activation(warm[:], q_raw[:, 0, 0:1], ACT.Exp, scale=0.0)
+        nc.scalar.activation(warm[:], ident[:, 0:1], ACT.Exp)
 
-        ks_g = sbuf("ks_g", [P, N], U8)
-        nc.vector.tensor_copy(ks_g[:], ks_pool[:].bitcast(U8).indirect(offsets[:]))
         vs_g = sbuf("vs_g", [P, N], F32)
         nc.vector.tensor_copy(vs_g[:], vs_pool[:].indirect(offsets[:]))
+        kw_g = sbuf("kw_g", [P, N], U32)
+        nc.vector.tensor_copy(kw_g[:], kw_pool[:].bitcast(U32).indirect(offsets[:]))
+        ks_g = sbuf("ks_g", [P, N], U8)
+        nc.vector.tensor_copy(ks_g[:], ks_pool[:].bitcast(U8).indirect(offsets[:]))
+        vs_col = sbuf("vs_col", [P, PACK], F32)
+        nc.sync.dma_start(vs_col[:], vs_g[P - 1 : P, :])
 
         q_bf = [sbuf(f"q_bf{b}", [P, P, PACK], BF16) for b in range(QB)]
         q_codes = [sbuf("q_codes0", [P, P], U32), shared("q_codes1", [P, P], U32, 4096)]
         q_scales = sbuf("q_scales", [P, NQ], U8)
-        kw_g = sbuf("kw_g", [P, N], U32)
         kb_g = shared("kb_g", [P, N], F32, 0)
 
         def quantise_queries(b):
@@ -88,11 +90,10 @@ def tile_attend_soft_kb_srtq256n512t1024_kernel(tc, qT, k_words, k_scales, vT, v
         for b in range(QB):
             nc.scalar.copy(q_bf[b][:], q_raw[:, :, cols(b)].rearrange("p j q -> p q j"))
         quantise_queries(0)
-        nc.vector.tensor_copy(kw_g[:], kw_pool[:].bitcast(U32).indirect(offsets[:]))
         quantise_queries(1)
         nc.vector.tensor_copy(kb_g[:], kb_pool[:].indirect(offsets[:]))
 
-        score_ps = [ps.tile([P, N], F32, name=f"score_ps{b}") for b in range(QB)]
+        score_ps = [ps.tile([P, N], F32, name=f"score_ps{b}", tag=f"bank{b}") for b in range(QB)]
         for b in range(QB):
             nc.tensor.matmul_mx(
                 out=score_ps[b][:],
@@ -103,10 +104,6 @@ def tile_attend_soft_kb_srtq256n512t1024_kernel(tc, qT, k_words, k_scales, vT, v
                 start=True,
                 stop=True,
             )
-
-        vs_ps = ps.tile([P, PACK, P], F32, name="vs_ps")
-        for t in range(PACK):
-            nc.tensor.transpose(vs_ps[:, t, :], vs_g[:, t:N:PACK], ident[:])
 
         v_bf = sbuf("v_bf", [P, T], BF16, tag="v_bf_then_p0")
         for half in halves:
@@ -124,8 +121,6 @@ def tile_attend_soft_kb_srtq256n512t1024_kernel(tc, qT, k_words, k_scales, vT, v
             nc.vector.tensor_tensor(s[b][:], score_ps[b][:], kb_g[:], ALU.add)
         for b in range(QB):
             nc.vector.tensor_reduce(neg_max[b][:], s[b][:], AX.X, ALU.max, negate=True)
-        vs_col = shared("vs_col", [P, PACK], F32, 0)
-        nc.vector.tensor_copy(vs_col[:], vs_ps[:, :, 0])
         v_k = shared("v_k", [P, DV, PACK], BF16, 64)
         nc.vector.tensor_copy(v_k[:].bitcast(F32), v_ps[:].rearrange("p u e -> p e u"))
         v_codes = sbuf("v_codes", [P, DV], U32)

@@ -56,10 +56,10 @@ def tile_attend_soft_kb_srtq256n512t1024_kernel(tc, qT, k_words, k_scales, vT, v
 
         nc.sync.dma_start(offsets[:], offs)
         nc.sync.dma_start(vs_pool[P - 1 : P, :], vs[0:1, :])
-        nc.sync.dma_start(kw_pool[:], k_words[0].rearrange("p n t -> p (n t)").bitcast(I32))
-        for quad in range(4):
-            nc.sync.dma_start(ks_pool[32 * quad : 32 * quad + 4, :], k_scales[0, 4 * quad : 4 * quad + 4, :].bitcast(I32))
         nc.sync.dma_start(q_raw[:], qT[0].rearrange("(p j) q -> p j q", j=PACK))
+        for quad in range(4):
+            nc.scalar.dma_start(ks_pool[32 * quad : 32 * quad + 4, :], k_scales[0, 4 * quad : 4 * quad + 4, :].bitcast(I32))
+        nc.sync.dma_start(kw_pool[:], k_words[0].rearrange("p n t -> p (n t)").bitcast(I32))
         nc.sync.dma_start(kb_pool[:], kb)
         for half in halves:
             nc.sync.dma_start(v_pool[:, half], vT[:, half])
@@ -68,8 +68,6 @@ def tile_attend_soft_kb_srtq256n512t1024_kernel(tc, qT, k_words, k_scales, vT, v
 
         vs_g = sbuf("vs_g", [P, N], F32)
         nc.vector.tensor_copy(vs_g[:], vs_pool[:].indirect(offsets[:]))
-        kw_g = sbuf("kw_g", [P, N], U32)
-        nc.vector.tensor_copy(kw_g[:], kw_pool[:].bitcast(U32).indirect(offsets[:]))
         ks_g = sbuf("ks_g", [P, N], U8)
         nc.vector.tensor_copy(ks_g[:], ks_pool[:].bitcast(U8).indirect(offsets[:]))
         vs_col = sbuf("vs_col", [P, PACK], F32)
@@ -78,6 +76,7 @@ def tile_attend_soft_kb_srtq256n512t1024_kernel(tc, qT, k_words, k_scales, vT, v
         q_bf = [sbuf(f"q_bf{b}", [P, P, PACK], BF16) for b in range(QB)]
         q_codes = [sbuf("q_codes0", [P, P], U32), shared("q_codes1", [P, P], U32, 4096)]
         q_scales = sbuf("q_scales", [P, NQ], U8)
+        kw_g = sbuf("kw_g", [P, N], U32)
         kb_g = shared("kb_g", [P, N], F32, 0)
 
         def quantise_queries(b):
@@ -90,6 +89,7 @@ def tile_attend_soft_kb_srtq256n512t1024_kernel(tc, qT, k_words, k_scales, vT, v
         for b in range(QB):
             nc.scalar.copy(q_bf[b][:], q_raw[:, :, cols(b)].rearrange("p j q -> p q j"))
         quantise_queries(0)
+        nc.vector.tensor_copy(kw_g[:], kw_pool[:].bitcast(U32).indirect(offsets[:]))
         quantise_queries(1)
         nc.vector.tensor_copy(kb_g[:], kb_pool[:].indirect(offsets[:]))
 

@@ -20,6 +20,7 @@ AX = mybir.AxisListType
 P = 128
 PACK = 4
 QB = NQ // P
+EARLY = 256
 
 
 def tile_attend_soft_kb_srtq256n512t1024_kernel(tc, qT, k_words, k_scales, vT, vs, kb, offs, out):
@@ -56,10 +57,13 @@ def tile_attend_soft_kb_srtq256n512t1024_kernel(tc, qT, k_words, k_scales, vT, v
 
         nc.sync.dma_start(offsets[:], offs)
         nc.sync.dma_start(vs_pool[P - 1 : P, :], vs[0:1, :])
-        nc.sync.dma_start(q_raw[:], qT[0].rearrange("(p j) q -> p j q", j=PACK))
+        words_hbm = k_words[0].rearrange("p n t -> p (n t)").bitcast(I32)
+        nc.sync.dma_start(kw_pool[:, :EARLY], words_hbm[:, :EARLY])
         for quad in range(4):
-            nc.scalar.dma_start(ks_pool[32 * quad : 32 * quad + 4, :], k_scales[0, 4 * quad : 4 * quad + 4, :].bitcast(I32))
-        nc.sync.dma_start(kw_pool[:], k_words[0].rearrange("p n t -> p (n t)").bitcast(I32))
+            queue = nc.sync if quad < 2 else nc.scalar
+            queue.dma_start(ks_pool[32 * quad : 32 * quad + 4, :], k_scales[0, 4 * quad : 4 * quad + 4, :].bitcast(I32))
+        nc.sync.dma_start(q_raw[:], qT[0].rearrange("(p j) q -> p j q", j=PACK))
+        nc.sync.dma_start(kw_pool[:, EARLY:], words_hbm[:, EARLY:])
         nc.sync.dma_start(kb_pool[:], kb)
         for half in halves:
             nc.sync.dma_start(v_pool[:, half], vT[:, half])

@@ -95,7 +95,9 @@ def tile_attend_soft_kb_srtq256n512t1024_kernel(tc, qT, k_words, k_scales, vT, v
         quantise_queries(0)
         nc.vector.tensor_copy(kw_g[:], kw_pool[:].bitcast(U32).indirect(offsets[:]))
         quantise_queries(1)
-        nc.vector.tensor_copy(kb_g[:], kb_pool[:].indirect(offsets[:]))
+        slot_halves = [slice(0, N // 2), slice(N // 2, N)]
+        for h in range(2):
+            nc.vector.tensor_copy(kb_g[:, slot_halves[h]], kb_pool[:].indirect(offsets[:, h * N // 32 : (h + 1) * N // 32]))
 
         score_ps = [ps.tile([P, N], F32, name=f"score_ps{b}", tag=f"bank{b}") for b in range(QB)]
         for b in range(QB):
@@ -121,8 +123,9 @@ def tile_attend_soft_kb_srtq256n512t1024_kernel(tc, qT, k_words, k_scales, vT, v
 
         s = [sbuf(f"s{b}", [P, N], F32) for b in range(QB)]
         neg_max = [shared("neg_max0", [P, 1], F32, 4096), sbuf("neg_max1", [P, 1], F32)]
-        for b in range(QB):
-            nc.vector.tensor_tensor(s[b][:], score_ps[b][:], kb_g[:], ALU.add)
+        for half in slot_halves:
+            nc.vector.tensor_tensor(s[0][:, half], score_ps[0][:, half], kb_g[:, half], ALU.add)
+        nc.vector.tensor_tensor(s[1][:], score_ps[1][:], kb_g[:], ALU.add)
         for b in range(QB):
             nc.vector.tensor_reduce(neg_max[b][:], s[b][:], AX.X, ALU.max, negate=True)
         v_k = shared("v_k", [P, DV, PACK], BF16, 64)

@@ -45,11 +45,10 @@ def tile_attend_soft_kb_srtq256n512t1024_kernel(tc, qT, k_words, k_scales, vT, v
         kw_pool = sbuf("kw_pool", [P, T], I32)
         ks_pool = sbuf("ks_pool", [P, T // 4], I32)
         kb_pool = sbuf("kb_pool", [P, T], F32)
-        v_pool = sbuf("v_pool", [P, T], F32)
+        v_pool = sbuf("v_pool", [P, T], F32, tag="v_pool_then_p0")
         vs_pool = sbuf("vs_pool", [P, T], F32)
         ident = sbuf("ident", [P, P], F32)
 
-        warm = sbuf("warm", [P, 1], F32)
         nc.vector.memset(ks_pool[:], 0)
         nc.vector.memset(vs_pool[0 : P - 1, :].bitcast(I32), 0)
         nc.vector.memset(ident[:], 0.0)
@@ -67,8 +66,6 @@ def tile_attend_soft_kb_srtq256n512t1024_kernel(tc, qT, k_words, k_scales, vT, v
         nc.sync.dma_start(kb_pool[:], kb)
         for half in halves:
             nc.sync.dma_start(v_pool[:, half], vT[:, half])
-
-        nc.scalar.activation(warm[:], ident[:, 0:1], ACT.Exp)
 
         vs_g = sbuf("vs_g", [P, N], F32)
         nc.vector.tensor_copy(vs_g[:], vs_pool[:].indirect(offsets[:]))
@@ -91,7 +88,7 @@ def tile_attend_soft_kb_srtq256n512t1024_kernel(tc, qT, k_words, k_scales, vT, v
             )
 
         for b in range(QB):
-            nc.scalar.copy(q_bf[b][:], q_raw[:, :, cols(b)].rearrange("p j q -> p q j"))
+            nc.scalar.activation(q_bf[b][:], q_raw[:, :, cols(b)].rearrange("p j q -> p q j"), ACT.Copy)
         quantise_queries(0)
         nc.vector.tensor_copy(kw_g[:], kw_pool[:].bitcast(U32).indirect(offsets[:]))
         quantise_queries(1)
@@ -111,7 +108,7 @@ def tile_attend_soft_kb_srtq256n512t1024_kernel(tc, qT, k_words, k_scales, vT, v
                 stop=True,
             )
 
-        v_bf = sbuf("v_bf", [P, T], BF16, tag="v_bf_then_p0")
+        v_bf = sbuf("v_bf", [P, T], BF16)
         for half in halves:
             nc.scalar.copy(v_bf[:, half], v_pool[:, half])
         v_g = sbuf("v_g", [P, N], BF16)
@@ -136,7 +133,7 @@ def tile_attend_soft_kb_srtq256n512t1024_kernel(tc, qT, k_words, k_scales, vT, v
             out=v_codes[:].bitcast(FP8X4), scales=v_scales[:], in_=v_k[:].rearrange("p e t -> p (e t)")
         )
 
-        p = [sbuf("p0", [P, PACK, P], F32, tag="v_bf_then_p0"), sbuf("p1", [P, PACK, P], F32)]
+        p = [sbuf("p0", [P, PACK, P], F32, tag="v_pool_then_p0"), sbuf("p1", [P, PACK, P], F32)]
         part_sum = sbuf("part_sum", [P, QB, 2], F32)
         p_ps = [ps.tile([P, PACK, P], F32, name=f"p_ps{b}") for b in range(QB)]
         for b in range(QB):

@@ -55,7 +55,7 @@ def tile_attend_soft_kb_srtq256n512t1024_kernel(tc, qT, k_words, k_scales, vT, v
         make_identity(nc, ident[:], nomemset=True)
 
         nc.sync.dma_start(offsets[:], offs)
-        nc.sync.dma_start(vs_pool[P - 1 : P, :], vs[0:1, :])
+        nc.scalar.dma_start(vs_pool[P - 1 : P, :], vs[0:1, :])
         words_hbm = k_words[0].rearrange("p n t -> p (n t)").bitcast(I32)
         nc.sync.dma_start(kw_pool[:, :EARLY], words_hbm[:, :EARLY])
         for quad in range(4):
@@ -88,7 +88,11 @@ def tile_attend_soft_kb_srtq256n512t1024_kernel(tc, qT, k_words, k_scales, vT, v
             )
 
         for b in range(QB):
-            nc.scalar.activation(q_bf[b][:], q_raw[:, :, cols(b)].rearrange("p j q -> p q j"), ACT.Copy)
+            nc.scalar.activation(
+                q_bf[b][:].rearrange("p (c i) j -> p c j i", i=4),
+                q_raw[:, :, cols(b)].rearrange("p j (c i) -> p c j i", i=4),
+                ACT.Copy,
+            )
         quantise_queries(0)
         nc.vector.tensor_copy(kw_g[:], kw_pool[:].bitcast(U32).indirect(offsets[:]))
         quantise_queries(1)

@@ -47,12 +47,9 @@ def tile_attend_soft_kb_srtq256n512t1024_kernel(tc, qT, k_words, k_scales, vT, v
         kb_pool = sbuf("kb_pool", [P, T], F32)
         v_pool = sbuf("v_pool", [P, T], F32, tag="v_pool_then_p0")
         vs_pool = sbuf("vs_pool", [P, T], F32)
-        ident = sbuf("ident", [P, P], F32)
 
         nc.vector.memset(ks_pool[:], 0)
         nc.vector.memset(vs_pool[0 : P - 1, :].bitcast(I32), 0)
-        nc.vector.memset(ident[:], 0.0)
-        make_identity(nc, ident[:], nomemset=True)
 
         nc.sync.dma_start(offsets[:], offs)
         nc.scalar.dma_start(vs_pool[P - 1 : P, :], vs[0:1, :])
@@ -99,6 +96,9 @@ def tile_attend_soft_kb_srtq256n512t1024_kernel(tc, qT, k_words, k_scales, vT, v
         slot_halves = [slice(0, N // 2), slice(N // 2, N)]
         for h in range(2):
             nc.vector.tensor_copy(kb_g[:, slot_halves[h]], kb_pool[:].indirect(offsets[:, h * N // 32 : (h + 1) * N // 32]))
+
+        ident = sbuf("ident", [P, P], F32, tag="kb_pool")
+        make_identity(nc, ident[:])
 
         score_ps = [ps.tile([P, N], F32, name=f"score_ps{b}", tag=f"bank{b}") for b in range(QB)]
         for b in range(QB):
@@ -156,7 +156,6 @@ def tile_attend_soft_kb_srtq256n512t1024_kernel(tc, qT, k_words, k_scales, vT, v
         w = [sbuf(f"w{b}", [P, P, PACK], BF16) for b in range(QB)]
         w_codes = [sbuf(f"w_codes{b}", [P, P], U32) for b in range(QB)]
         w_scales = [sbuf(f"w_scales{b}", [P, P], U8) for b in range(QB)]
-        row_sum = sbuf("row_sum", [P, QB], F32)
         inv_sum = sbuf("inv_sum", [P, QB], F32)
 
         def weigh(b):
@@ -176,6 +175,7 @@ def tile_attend_soft_kb_srtq256n512t1024_kernel(tc, qT, k_words, k_scales, vT, v
         weigh(1)
         quantise_weights(0)
         quantise_weights(1)
+        row_sum = sbuf("row_sum", [P, QB], F32, tag="v_pool_then_p0")
         nc.vector.tensor_reduce(row_sum[:], part_sum[:], AX.X, ALU.add)
         nc.vector.reciprocal(inv_sum[:], row_sum[:])
 

@@ -20,7 +20,7 @@ AX = mybir.AxisListType
 P = 128
 PACK = 4
 QB = NQ // P
-EARLY = 256
+EARLY = 512
 
 
 def tile_attend_soft_kb_srtq256n512t1024_kernel(tc, qT, k_words, k_scales, vT, vs, kb, offs, out):
@@ -52,7 +52,7 @@ def tile_attend_soft_kb_srtq256n512t1024_kernel(tc, qT, k_words, k_scales, vT, v
         nc.vector.memset(vs_pool[0 : P - 1, :].bitcast(I32), 0)
 
         nc.sync.dma_start(offsets[:], offs)
-        nc.scalar.dma_start(vs_pool[P - 1 : P, :], vs[0:1, :])
+        nc.sync.dma_start(vs_pool[P - 1 : P, :], vs[0:1, :])
         words_hbm = k_words[0].rearrange("p n t -> p (n t)").bitcast(I32)
         nc.sync.dma_start(kw_pool[:, :EARLY], words_hbm[:, :EARLY])
         for quad in range(4):

@@ -191,8 +191,5 @@ def tile_attend_soft_kb_srtq256n512t1024_kernel(tc, qT, k_words, k_scales, vT, v
                 stop=True,
             )
             y = sbuf(f"y{b}", [P, DV], F32)
-            if b == 0:
-                nc.scalar.activation(y[:], y_ps[:], ACT.Copy, scale=inv_sum[:, b : b + 1])
-            else:
-                nc.vector.tensor_scalar(y[:], y_ps[:], inv_sum[:, b : b + 1], None, ALU.mult)
+            nc.vector.tensor_scalar(y[:], y_ps[:], inv_sum[:, b : b + 1], None, ALU.mult)
             nc.sync.dma_start(out[0, cols(b), :], y[:])

@@ -21,6 +21,7 @@ P = 128
 PACK = 4
 QB = NQ // P
 EARLY = 512
+KB_SCALAR = 160
 
 
 def tile_attend_soft_kb_srtq256n512t1024_kernel(tc, qT, k_words, k_scales, vT, vs, kb, offs, out):
@@ -41,7 +42,10 @@ def tile_attend_soft_kb_srtq256n512t1024_kernel(tc, qT, k_words, k_scales, vT, v
 
         halves = [slice(0, T // 2), slice(T // 2, T)]
         offsets = sb.tile([P, N // 16], U16, name="offsets")
-        q_raw = shared("q_raw", [P, PACK, NQ], F32, 0)
+        staged = sbuf("staged", [P, PACK * NQ + KB_SCALAR], F32)
+        q_raw = staged[:, : PACK * NQ].rearrange("p (j q) -> p j q", j=PACK)
+        kb_g = staged[:, PACK * NQ + KB_SCALAR - N :]
+        v_k = kb_g[:, : N // 2]
         kw_pool = sbuf("kw_pool", [P, T], I32)
         ks_pool = sbuf("ks_pool", [P, T // 4], I32)
         kb_pool = sbuf("kb_pool", [P, T], F32)
@@ -58,7 +62,7 @@ def tile_attend_soft_kb_srtq256n512t1024_kernel(tc, qT, k_words, k_scales, vT, v
         for quad in range(4):
             queue = nc.sync if quad < 2 else nc.scalar
             queue.dma_start(ks_pool[32 * quad : 32 * quad + 4, :], k_scales[0, 4 * quad : 4 * quad + 4, :].bitcast(I32))
-        nc.sync.dma_start(q_raw[:], qT[0].rearrange("(p j) q -> p j q", j=PACK))
+        nc.sync.dma_start(q_raw, qT[0].rearrange("(p j) q -> p j q", j=PACK))
         nc.sync.dma_start(kw_pool[:, EARLY:], words_hbm[:, EARLY:])
         nc.sync.dma_start(kb_pool[:], kb)
         for half in halves:
@@ -75,7 +79,6 @@ def tile_attend_soft_kb_srtq256n512t1024_kernel(tc, qT, k_words, k_scales, vT, v
         q_codes = [sbuf("q_codes0", [P, P], U32), shared("q_codes1", [P, P], U32, 4096)]
         q_scales = sbuf("q_scales", [P, NQ], U8)
         kw_g = sbuf("kw_g", [P, N], U32)
-        kb_g = shared("kb_g", [P, N], F32, 0)
 
         def quantise_queries(b):
             nc.vector.quantize_mx(
@@ -94,8 +97,10 @@ def tile_attend_soft_kb_srtq256n512t1024_kernel(tc, qT, k_words, k_scales, vT, v
         nc.vector.tensor_copy(kw_g[:], kw_pool[:].bitcast(U32).indirect(offsets[:]))
         quantise_queries(1)
         slot_halves = [slice(0, N // 2), slice(N // 2, N)]
-        for h in range(2):
-            nc.vector.tensor_copy(kb_g[:, slot_halves[h]], kb_pool[:].indirect(offsets[:, h * N // 32 : (h + 1) * N // 32]))
+        split = N - KB_SCALAR
+        nc.scalar.activation(kb_g[:, split:], kb_pool[:].indirect(offsets[:, split // 16 :]), ACT.Copy)
+        for first, last in ((0, N // 2), (N // 2, split)):
+            nc.vector.tensor_copy(kb_g[:, first:last], kb_pool[:].indirect(offsets[:, first // 16 : last // 16]))
 
         ident = sbuf("ident", [P, P], F32, tag="kb_pool")
         make_identity(nc, ident[:])
@@ -126,15 +131,14 @@ def tile_attend_soft_kb_srtq256n512t1024_kernel(tc, qT, k_words, k_scales, vT, v
         neg_max = [shared("neg_max0", [P, 1], F32, 4096), sbuf("neg_max1", [P, 1], F32)]
         for half in slot_halves:
             nc.vector.tensor_tensor(s[0][:, half], score_ps[0][:, half], kb_g[:, half], ALU.add)
-        nc.vector.tensor_tensor(s[1][:], score_ps[1][:], kb_g[:], ALU.add)
+        nc.vector.tensor_tensor(s[1][:], score_ps[1][:], kb_g, ALU.add)
         for b in range(QB):
             nc.vector.tensor_reduce(neg_max[b][:], s[b][:], AX.X, ALU.max, negate=True)
-        v_k = shared("v_k", [P, DV, PACK], BF16, 64)
-        nc.vector.tensor_copy(v_k[:].bitcast(F32), v_ps[:].rearrange("p u e -> p e u"))
+        nc.vector.tensor_copy(v_k.rearrange("p (e u) -> p e u", u=2), v_ps[:].rearrange("p u e -> p e u"))
         v_codes = sbuf("v_codes", [P, DV], U32)
         v_scales = sbuf("v_scales", [P, DV], U8)
         nc.vector.quantize_mx(
-            out=v_codes[:].bitcast(FP8X4), scales=v_scales[:], in_=v_k[:].rearrange("p e t -> p (e t)")
+            out=v_codes[:].bitcast(FP8X4), scales=v_scales[:], in_=v_k.bitcast(BF16)
         )
 
         p = [sbuf("p0", [P, PACK, P], F32, tag="v_pool_then_p0"), sbuf("p1", [P, PACK, P], F32)]

@@ -21,7 +21,8 @@ P = 128
 PACK = 4
 QB = NQ // P
 EARLY = 512
-KB_SCALAR = 160
+KB_SCALAR = 128
+V_GPSIMD = 256
 
 
 def tile_attend_soft_kb_srtq256n512t1024_kernel(tc, qT, k_words, k_scales, vT, vs, kb, offs, out):
@@ -118,8 +119,9 @@ def tile_attend_soft_kb_srtq256n512t1024_kernel(tc, qT, k_words, k_scales, vT, v
             )
 
         v_bf = sbuf("v_bf", [P, T], BF16)
-        for half in halves:
-            nc.scalar.copy(v_bf[:, half], v_pool[:, half])
+        for part in (slice(0, T // 2), slice(T // 2, T - V_GPSIMD)):
+            nc.scalar.copy(v_bf[:, part], v_pool[:, part])
+        nc.gpsimd.tensor_copy(v_bf[:, T - V_GPSIMD :], v_pool[:, T - V_GPSIMD :])
         v_g = sbuf("v_g", [P, N], BF16)
         nc.scalar.activation(v_g[:], v_bf[:].indirect(offsets[:]), ACT.Copy)
         v_ps = ps.tile([P, 2, P], F32, name="v_ps")

@@ -22,7 +22,8 @@ PACK = 4
 QB = NQ // P
 EARLY = 512
 KB_SCALAR = 128
-V_GPSIMD = 256
+PREFIX = T - N // 2
+BLOCK = 32
 
 
 def tile_attend_soft_kb_srtq256n512t1024_kernel(tc, qT, k_words, k_scales, vT, vs, kb, offs, out):
@@ -40,6 +41,12 @@ def tile_attend_soft_kb_srtq256n512t1024_kernel(tc, qT, k_words, k_scales, vT, v
 
         def cols(b):
             return slice(b * P, (b + 1) * P)
+
+        def woven(ap):
+            return ap.rearrange("p (g h x) -> p h g x", h=2, x=BLOCK)
+
+        def listed(ap):
+            return ap.rearrange("p (h g x) -> p h g x", h=2, x=BLOCK)
 
         halves = [slice(0, T // 2), slice(T // 2, T)]
         offsets = sb.tile([P, N // 16], U16, name="offsets")
@@ -70,7 +77,7 @@ def tile_attend_soft_kb_srtq256n512t1024_kernel(tc, qT, k_words, k_scales, vT, v
             nc.sync.dma_start(v_pool[:, half], vT[:, half])
 
         vs_g = sbuf("vs_g", [P, N], F32)
-        nc.vector.tensor_copy(vs_g[:], vs_pool[:].indirect(offsets[:]))
+        nc.vector.tensor_copy(woven(vs_g[:]), vs_pool[:].indirect(offsets[:]))
         ks_g = sbuf("ks_g", [P, N], U8)
         nc.vector.tensor_copy(ks_g[:], ks_pool[:].bitcast(U8).indirect(offsets[:]))
         vs_col = sbuf("vs_col", [P, PACK], F32)
@@ -97,7 +104,6 @@ def tile_attend_soft_kb_srtq256n512t1024_kernel(tc, qT, k_words, k_scales, vT, v
         quantise_queries(0)
         nc.vector.tensor_copy(kw_g[:], kw_pool[:].bitcast(U32).indirect(offsets[:]))
         quantise_queries(1)
-        slot_halves = [slice(0, N // 2), slice(N // 2, N)]
         split = N - KB_SCALAR
         nc.scalar.activation(kb_g[:, split:], kb_pool[:].indirect(offsets[:, split // 16 :]), ACT.Copy)
         for first, last in ((0, N // 2), (N // 2, split)):
@@ -119,11 +125,12 @@ def tile_attend_soft_kb_srtq256n512t1024_kernel(tc, qT, k_words, k_scales, vT, v
             )
 
         v_bf = sbuf("v_bf", [P, T], BF16)
-        for part in (slice(0, T // 2), slice(T // 2, T - V_GPSIMD)):
+        for part in (slice(0, T // 2), slice(T // 2, PREFIX)):
             nc.scalar.copy(v_bf[:, part], v_pool[:, part])
-        nc.gpsimd.tensor_copy(v_bf[:, T - V_GPSIMD :], v_pool[:, T - V_GPSIMD :])
+        nc.gpsimd.tensor_copy(v_bf[:, PREFIX:], v_pool[:, PREFIX:])
         v_g = sbuf("v_g", [P, N], BF16)
-        nc.scalar.activation(v_g[:], v_bf[:].indirect(offsets[:]), ACT.Copy)
+        for h, window in enumerate((v_bf[:, :PREFIX], v_bf[:])):
+            nc.scalar.activation(woven(v_g[:])[:, h], window.indirect(offsets[:, h * N // 32 : (h + 1) * N // 32]), ACT.Copy)
         v_ps = ps.tile([P, 2, P], F32, name="v_ps")
         v_words = v_g[:].bitcast(F32)
         for u in range(2):
@@ -131,9 +138,9 @@ def tile_attend_soft_kb_srtq256n512t1024_kernel(tc, qT, k_words, k_scales, vT, v
 
         s = [sbuf(f"s{b}", [P, N], F32) for b in range(QB)]
         neg_max = [shared("neg_max0", [P, 1], F32, 4096), sbuf("neg_max1", [P, 1], F32)]
-        for half in slot_halves:
-            nc.vector.tensor_tensor(s[0][:, half], score_ps[0][:, half], kb_g[:, half], ALU.add)
-        nc.vector.tensor_tensor(s[1][:], score_ps[1][:], kb_g, ALU.add)
+        for h in range(2):
+            nc.vector.tensor_tensor(woven(s[0][:])[:, h], listed(score_ps[0][:])[:, h], listed(kb_g)[:, h], ALU.add)
+        nc.vector.tensor_tensor(woven(s[1][:]), listed(score_ps[1][:]), listed(kb_g), ALU.add)
         for b in range(QB):
             nc.vector.tensor_reduce(neg_max[b][:], s[b][:], AX.X, ALU.max, negate=True)
         nc.vector.tensor_copy(v_k.rearrange("p (e u) -> p e u", u=2), v_ps[:].rearrange("p u e -> p e u"))

@@ -21,7 +21,7 @@ P = 128
 PACK = 4
 QB = NQ // P
 EARLY = 512
-KB_SCALAR = 128
+KB_SCALAR = 192
 PREFIX = T - N // 2
 BLOCK = 32
 

@@ -112,17 +112,19 @@ def tile_attend_soft_kb_srtq256n512t1024_kernel(tc, qT, k_words, k_scales, vT, v
         ident = sbuf("ident", [P, P], F32, tag="kb_pool")
         make_identity(nc, ident[:])
 
-        score_ps = [ps.tile([P, N], F32, name=f"score_ps{b}", tag=f"bank{b}") for b in range(QB)]
+        score_ps = [[ps.tile([P, N // 2], F32, name=f"score_ps{b}{h}") for h in range(2)] for b in range(QB)]
         for b in range(QB):
-            nc.tensor.matmul_mx(
-                out=score_ps[b][:],
-                lhsT=q_codes[b][:].bitcast(FP8X4),
-                lhsT_scale=q_scales[:, cols(b)],
-                rhs=kw_g[:].bitcast(FP8X4),
-                rhs_scale=ks_g[:],
-                start=True,
-                stop=True,
-            )
+            for h in range(2):
+                slots = slice(h * N // 2, (h + 1) * N // 2)
+                nc.tensor.matmul_mx(
+                    out=score_ps[b][h][:],
+                    lhsT=q_codes[b][:].bitcast(FP8X4),
+                    lhsT_scale=q_scales[:, cols(b)],
+                    rhs=kw_g[:, slots].bitcast(FP8X4),
+                    rhs_scale=ks_g[:, slots],
+                    start=True,
+                    stop=True,
+                )
 
         v_bf = sbuf("v_bf", [P, T], BF16)
         for part in (slice(0, T // 2), slice(T // 2, PREFIX)):
@@ -138,9 +140,10 @@ def tile_attend_soft_kb_srtq256n512t1024_kernel(tc, qT, k_words, k_scales, vT, v
 
         s = [sbuf(f"s{b}", [P, N], F32) for b in range(QB)]
         neg_max = [shared("neg_max0", [P, 1], F32, 4096), sbuf("neg_max1", [P, 1], F32)]
-        for h in range(2):
-            nc.vector.tensor_tensor(woven(s[0][:])[:, h], listed(score_ps[0][:])[:, h], listed(kb_g)[:, h], ALU.add)
-        nc.vector.tensor_tensor(woven(s[1][:]), listed(score_ps[1][:]), listed(kb_g), ALU.add)
+        for b in range(QB):
+            for h in range(2):
+                scores = score_ps[b][h][:].rearrange("p (g x) -> p g x", x=BLOCK)
+                nc.vector.tensor_tensor(woven(s[b][:])[:, h], scores, listed(kb_g)[:, h], ALU.add)
         for b in range(QB):
             nc.vector.tensor_reduce(neg_max[b][:], s[b][:], AX.X, ALU.max, negate=True)
         nc.vector.tensor_copy(v_k.rearrange("p (e u) -> p e u", u=2), v_ps[:].rearrange("p u e -> p e u"))
@@ -193,7 +196,7 @@ def tile_attend_soft_kb_srtq256n512t1024_kernel(tc, qT, k_words, k_scales, vT, v
         nc.vector.reciprocal(inv_sum[:], row_sum[:])
 
         for b in range(QB):
-            y_ps = ps.tile([P, DV], F32, name=f"y_ps{b}")
+            y_ps = ps.tile([P, DV], F32, name=f"y_ps{b}", tag=f"score_ps{b}0")
             nc.tensor.matmul_mx(
                 out=y_ps[:],
                 lhsT=w_codes[b][:].bitcast(FP8X4),

@@ -23,7 +23,7 @@ QB = NQ // P
 EARLY = 512
 KB_SCALAR = 192
 PREFIX = T - N // 2
-BLOCK = 32
+RUN = 8
 
 
 def tile_attend_soft_kb_srtq256n512t1024_kernel(tc, qT, k_words, k_scales, vT, vs, kb, offs, out):
@@ -41,12 +41,6 @@ def tile_attend_soft_kb_srtq256n512t1024_kernel(tc, qT, k_words, k_scales, vT, v
 
         def cols(b):
             return slice(b * P, (b + 1) * P)
-
-        def woven(ap):
-            return ap.rearrange("p (g h x) -> p h g x", h=2, x=BLOCK)
-
-        def listed(ap):
-            return ap.rearrange("p (h g x) -> p h g x", h=2, x=BLOCK)
 
         halves = [slice(0, T // 2), slice(T // 2, T)]
         offsets = sb.tile([P, N // 16], U16, name="offsets")
@@ -77,7 +71,7 @@ def tile_attend_soft_kb_srtq256n512t1024_kernel(tc, qT, k_words, k_scales, vT, v
             nc.sync.dma_start(v_pool[:, half], vT[:, half])
 
         vs_g = sbuf("vs_g", [P, N], F32)
-        nc.vector.tensor_copy(woven(vs_g[:]), vs_pool[:].indirect(offsets[:]))
+        nc.vector.tensor_copy(vs_g[:].rearrange("p (m r u e) -> p m u r e", r=RUN // 2, u=2, e=2), vs_pool[:].indirect(offsets[:]))
         ks_g = sbuf("ks_g", [P, N], U8)
         nc.vector.tensor_copy(ks_g[:], ks_pool[:].bitcast(U8).indirect(offsets[:]))
         vs_col = sbuf("vs_col", [P, PACK], F32)
@@ -132,26 +126,34 @@ def tile_attend_soft_kb_srtq256n512t1024_kernel(tc, qT, k_words, k_scales, vT, v
         nc.gpsimd.tensor_copy(v_bf[:, PREFIX:], v_pool[:, PREFIX:])
         v_g = sbuf("v_g", [P, N], BF16)
         for h, window in enumerate((v_bf[:, :PREFIX], v_bf[:])):
-            nc.scalar.activation(woven(v_g[:])[:, h], window.indirect(offsets[:, h * N // 32 : (h + 1) * N // 32]), ACT.Copy)
+            runs = v_g[:].rearrange("p (u m x) -> p m u x", u=2, x=RUN)[:, h * 16 : (h + 1) * 16]
+            nc.scalar.activation(runs, window.indirect(offsets[:, h * N // 32 : (h + 1) * N // 32]), ACT.Copy)
         v_ps = ps.tile([P, 2, P], F32, name="v_ps")
         v_words = v_g[:].bitcast(F32)
         for u in range(2):
-            nc.tensor.transpose(v_ps[:, u, :], v_words[:, u : N // 2 : 2], ident[:])
+            nc.tensor.transpose(v_ps[:, u, :], v_words[:, cols(u)], ident[:])
 
         s = [sbuf(f"s{b}", [P, N], F32) for b in range(QB)]
         neg_max = [shared("neg_max0", [P, 1], F32, 4096), sbuf("neg_max1", [P, 1], F32)]
         for b in range(QB):
             for h in range(2):
-                scores = score_ps[b][h][:].rearrange("p (g x) -> p g x", x=BLOCK)
-                nc.vector.tensor_tensor(woven(s[b][:])[:, h], scores, listed(kb_g)[:, h], ALU.add)
+                slots = slice(h * N // 2, (h + 1) * N // 2)
+                nc.vector.tensor_tensor(s[b][:, slots], score_ps[b][h][:], kb_g[:, slots], ALU.add)
         for b in range(QB):
             nc.vector.tensor_reduce(neg_max[b][:], s[b][:], AX.X, ALU.max, negate=True)
-        nc.vector.tensor_copy(v_k.rearrange("p (e u) -> p e u", u=2), v_ps[:].rearrange("p u e -> p e u"))
+        features = [slice(0, DV // 2), slice(DV // 2, DV)]
+        for part in features:
+            nc.vector.tensor_copy(
+                v_k.rearrange("p (e u) -> p e u", u=2)[:, part], v_ps[:, :, part].rearrange("p u e -> p e u")
+            )
         v_codes = sbuf("v_codes", [P, DV], U32)
         v_scales = sbuf("v_scales", [P, DV], U8)
-        nc.vector.quantize_mx(
-            out=v_codes[:].bitcast(FP8X4), scales=v_scales[:], in_=v_k.bitcast(BF16)
-        )
+        for part in features:
+            nc.vector.quantize_mx(
+                out=v_codes[:, part].bitcast(FP8X4),
+                scales=v_scales[:, part],
+                in_=v_k[:, 2 * part.start : 2 * part.stop].bitcast(BF16),
+            )
 
         p = [sbuf("p0", [P, PACK, P], F32, tag="v_pool_then_p0"), sbuf("p1", [P, PACK, P], F32)]
         part_sum = sbuf("part_sum", [P, QB, 2], F32)
@@ -160,8 +162,8 @@ def tile_attend_soft_kb_srtq256n512t1024_kernel(tc, qT, k_words, k_scales, vT, v
             for h in range(2):
                 places = slice(2 * h, 2 * h + 2)
                 nc.scalar.activation(
-                    p[b][:, places, :].rearrange("p t s -> p s t"),
-                    s[b][:].rearrange("p (s t) -> p s t", t=PACK)[:, :, places],
+                    p[b][:, places, :].rearrange("p e (m r) -> p e m r", r=RUN // 2),
+                    s[b][:].rearrange("p (m u r e) -> p u e m r", u=2, r=RUN // 2, e=2)[:, h],
                     ACT.Exp,
                     bias=neg_max[b][:],
                     accum_out=part_sum[:, b, h : h + 1],
@@ -174,23 +176,26 @@ def tile_attend_soft_kb_srtq256n512t1024_kernel(tc, qT, k_words, k_scales, vT, v
         w_scales = [sbuf(f"w_scales{b}", [P, P], U8) for b in range(QB)]
         inv_sum = sbuf("inv_sum", [P, QB], F32)
 
-        def weigh(b):
+        def weigh(b, queries):
             nc.vector.tensor_tensor(
-                w[b][:],
-                p_ps[b][:].rearrange("p t q -> p q t"),
-                vs_col[:].unsqueeze(1).to_broadcast([P, P, PACK]),
+                w[b][:, queries, :],
+                p_ps[b][:, :, queries].rearrange("p t q -> p q t"),
+                vs_col[:].unsqueeze(1).to_broadcast([P, queries.stop - queries.start, PACK]),
                 ALU.mult,
             )
 
-        def quantise_weights(b):
+        def quantise_weights(b, queries):
             nc.vector.quantize_mx(
-                out=w_codes[b][:].bitcast(FP8X4), scales=w_scales[b][:], in_=w[b][:].rearrange("p q t -> p (q t)")
+                out=w_codes[b][:, queries].bitcast(FP8X4),
+                scales=w_scales[b][:, queries],
+                in_=w[b][:, queries, :].rearrange("p q t -> p (q t)"),
             )
 
-        weigh(0)
-        weigh(1)
-        quantise_weights(0)
-        quantise_weights(1)
+        pieces = [(0, slice(0, P)), (1, slice(0, P // 2)), (1, slice(P // 2, P))]
+        for b, queries in pieces:
+            weigh(b, queries)
+        for b, queries in pieces:
+            quantise_weights(b, queries)
         row_sum = sbuf("row_sum", [P, QB], F32, tag="v_pool_then_p0")
         nc.vector.tensor_reduce(row_sum[:], part_sum[:], AX.X, ALU.add)
         nc.vector.reciprocal(inv_sum[:], row_sum[:])

@@ -22,6 +22,7 @@ PACK = 4
 QB = NQ // P
 EARLY = 512
 KB_SCALAR = 192
+KB_FIRST = 192
 PREFIX = T - N // 2
 RUN = 8
 
@@ -100,7 +101,7 @@ def tile_attend_soft_kb_srtq256n512t1024_kernel(tc, qT, k_words, k_scales, vT, v
         quantise_queries(1)
         split = N - KB_SCALAR
         nc.scalar.activation(kb_g[:, split:], kb_pool[:].indirect(offsets[:, split // 16 :]), ACT.Copy)
-        for first, last in ((0, N // 2), (N // 2, split)):
+        for first, last in ((0, KB_FIRST), (KB_FIRST, split)):
             nc.vector.tensor_copy(kb_g[:, first:last], kb_pool[:].indirect(offsets[:, first // 16 : last // 16]))
 
         ident = sbuf("ident", [P, P], F32, tag="kb_pool")
@@ -136,9 +137,11 @@ def tile_attend_soft_kb_srtq256n512t1024_kernel(tc, qT, k_words, k_scales, vT, v
         s = [sbuf(f"s{b}", [P, N], F32) for b in range(QB)]
         neg_max = [shared("neg_max0", [P, 1], F32, 4096), sbuf("neg_max1", [P, 1], F32)]
         for b in range(QB):
-            for h in range(2):
-                slots = slice(h * N // 2, (h + 1) * N // 2)
-                nc.vector.tensor_tensor(s[b][:, slots], score_ps[b][h][:], kb_g[:, slots], ALU.add)
+            cuts = [0, KB_FIRST, N // 2, N] if b == 0 else [0, N // 2, N]
+            for first, last in zip(cuts, cuts[1:]):
+                h, start = divmod(first, N // 2)
+                scores = score_ps[b][h][:, start : start + last - first]
+                nc.vector.tensor_tensor(s[b][:, first:last], scores, kb_g[:, first:last], ALU.add)
         for b in range(QB):
             nc.vector.tensor_reduce(neg_max[b][:], s[b][:], AX.X, ALU.max, negate=True)
         features = [slice(0, DV // 2), slice(DV // 2, DV)]
@@ -174,7 +177,7 @@ def tile_attend_soft_kb_srtq256n512t1024_kernel(tc, qT, k_words, k_scales, vT, v
         w = [sbuf(f"w{b}", [P, P, PACK], BF16) for b in range(QB)]
         w_codes = [sbuf(f"w_codes{b}", [P, P], U32) for b in range(QB)]
         w_scales = [sbuf(f"w_scales{b}", [P, P], U8) for b in range(QB)]
-        inv_sum = sbuf("inv_sum", [P, QB], F32)
+        inv_sum = sbuf("inv_sum", [P, QB], F32, tag="w0")
 
         def weigh(b, queries):
             nc.vector.tensor_tensor(
@@ -196,8 +199,8 @@ def tile_attend_soft_kb_srtq256n512t1024_kernel(tc, qT, k_words, k_scales, vT, v
             weigh(b, queries)
         for b, queries in pieces:
             quantise_weights(b, queries)
-        row_sum = sbuf("row_sum", [P, QB], F32, tag="v_pool_then_p0")
-        nc.vector.tensor_reduce(row_sum[:], part_sum[:], AX.X, ALU.add)
+        row_sum = sbuf("row_sum", [P, QB], F32)
+        nc.gpsimd.tensor_tensor(row_sum[:], part_sum[:, :, 0], part_sum[:, :, 1], ALU.add)
         nc.vector.reciprocal(inv_sum[:], row_sum[:])
 
         for b in range(QB):

@@ -122,19 +122,21 @@ def tile_attend_soft_kb_srtq256n512t1024_kernel(tc, qT, k_words, k_scales, vT, v
                 )
 
         v_bf = sbuf("v_bf", [P, T], BF16)
-        for part in (slice(0, T // 2), slice(T // 2, PREFIX)):
-            nc.scalar.copy(v_bf[:, part], v_pool[:, part])
+        for first, last in ((0, T // 2), (T // 2, T - 3 * N // 4), (T - 3 * N // 4, PREFIX)):
+            nc.scalar.copy(v_bf[:, first:last], v_pool[:, first:last])
         nc.gpsimd.tensor_copy(v_bf[:, PREFIX:], v_pool[:, PREFIX:])
         v_g = sbuf("v_g", [P, N], BF16)
-        for h, window in enumerate((v_bf[:, :PREFIX], v_bf[:])):
-            runs = v_g[:].rearrange("p (u m x) -> p m u x", u=2, x=RUN)[:, h * 16 : (h + 1) * 16]
-            nc.scalar.activation(runs, window.indirect(offsets[:, h * N // 32 : (h + 1) * N // 32]), ACT.Copy)
+        for first, last in ((0, N // 4), (N // 4, N // 2), (N // 2, N)):
+            runs = v_g[:].rearrange("p (u m x) -> p m u x", u=2, x=RUN)[:, first // 16 : last // 16]
+            window = v_bf[:, : T - N + last]
+            nc.scalar.activation(runs, window.indirect(offsets[:, first // 16 : last // 16]), ACT.Copy)
         v_ps = ps.tile([P, 2, P], F32, name="v_ps")
         v_words = v_g[:].bitcast(F32)
         for u in range(2):
             nc.tensor.transpose(v_ps[:, u, :], v_words[:, cols(u)], ident[:])
 
-        s = [sbuf(f"s{b}", [P, N], F32) for b in range(QB)]
+        s_both = sbuf("s_both", [P, QB * N], F32)
+        s = [s_both[:, b * N : (b + 1) * N] for b in range(QB)]
         neg_max = [shared("neg_max0", [P, 1], F32, 4096), sbuf("neg_max1", [P, 1], F32)]
         for b in range(QB):
             cuts = [0, KB_FIRST, N // 2, N] if b == 0 else [0, N // 2, N]
@@ -143,7 +145,7 @@ def tile_attend_soft_kb_srtq256n512t1024_kernel(tc, qT, k_words, k_scales, vT, v
                 scores = score_ps[b][h][:, start : start + last - first]
                 nc.vector.tensor_tensor(s[b][:, first:last], scores, kb_g[:, first:last], ALU.add)
         for b in range(QB):
-            nc.vector.tensor_reduce(neg_max[b][:], s[b][:], AX.X, ALU.max, negate=True)
+            nc.vector.tensor_reduce(neg_max[b][:], s[b], AX.X, ALU.max, negate=True)
         features = [slice(0, DV // 2), slice(DV // 2, DV)]
         for part in features:
             nc.vector.tensor_copy(
@@ -159,48 +161,51 @@ def tile_attend_soft_kb_srtq256n512t1024_kernel(tc, qT, k_words, k_scales, vT, v
             )
 
         p = [sbuf("p0", [P, PACK, P], F32, tag="v_pool_then_p0"), sbuf("p1", [P, PACK, P], F32)]
-        part_sum = sbuf("part_sum", [P, QB, 2], F32)
         p_ps = [ps.tile([P, PACK, P], F32, name=f"p_ps{b}") for b in range(QB)]
         for b in range(QB):
-            for h in range(2):
-                places = slice(2 * h, 2 * h + 2)
+            for t in range(PACK):
                 nc.scalar.activation(
-                    p[b][:, places, :].rearrange("p e (m r) -> p e m r", r=RUN // 2),
-                    s[b][:].rearrange("p (m u r e) -> p u e m r", u=2, r=RUN // 2, e=2)[:, h],
+                    p[b][:, t, :].rearrange("p (m r) -> p m r", r=RUN // 2),
+                    s[b].rearrange("p (m u r e) -> p u e m r", u=2, r=RUN // 2, e=2)[:, t // 2, t % 2],
                     ACT.Exp,
                     bias=neg_max[b][:],
-                    accum_out=part_sum[:, b, h : h + 1],
                 )
-            for t in range(PACK):
                 nc.tensor.transpose(p_ps[b][:, t, :], p[b][:, t, :], ident[:])
 
-        w = [sbuf(f"w{b}", [P, P, PACK], BF16) for b in range(QB)]
+        row_sum = sbuf("row_sum", [P, QB], F32)
+        for b in range(QB):
+            nc.scalar.activation(
+                s_both[:].rearrange("p (m u x) -> p u m x", u=2, x=RUN)[:, b],
+                p[b][:].rearrange("p t (m x) -> p (t m) x", x=RUN),
+                ACT.Copy,
+                accum_out=row_sum[:, b : b + 1],
+            )
+
+        pieces = [(0, slice(0, P)), (1, slice(0, P // 2)), (1, slice(P // 2, P))]
+        w = [sbuf(f"w{i}", [P, queries.stop - queries.start, PACK], BF16) for i, (b, queries) in enumerate(pieces)]
         w_codes = [sbuf(f"w_codes{b}", [P, P], U32) for b in range(QB)]
         w_scales = [sbuf(f"w_scales{b}", [P, P], U8) for b in range(QB)]
-        inv_sum = sbuf("inv_sum", [P, QB], F32, tag="w0")
+        inv_sum = sbuf("inv_sum", [P, QB], F32, tag="w1")
 
-        def weigh(b, queries):
+        def weigh(i, b, queries):
             nc.vector.tensor_tensor(
-                w[b][:, queries, :],
+                w[i][:],
                 p_ps[b][:, :, queries].rearrange("p t q -> p q t"),
                 vs_col[:].unsqueeze(1).to_broadcast([P, queries.stop - queries.start, PACK]),
                 ALU.mult,
             )
 
-        def quantise_weights(b, queries):
+        def quantise_weights(i, b, queries):
             nc.vector.quantize_mx(
                 out=w_codes[b][:, queries].bitcast(FP8X4),
                 scales=w_scales[b][:, queries],
-                in_=w[b][:, queries, :].rearrange("p q t -> p (q t)"),
+                in_=w[i][:].rearrange("p q t -> p (q t)"),
             )
 
-        pieces = [(0, slice(0, P)), (1, slice(0, P // 2)), (1, slice(P // 2, P))]
-        for b, queries in pieces:
-            weigh(b, queries)
-        for b, queries in pieces:
-            quantise_weights(b, queries)
-        row_sum = sbuf("row_sum", [P, QB], F32)
-        nc.gpsimd.tensor_tensor(row_sum[:], part_sum[:, :, 0], part_sum[:, :, 1], ALU.add)
+        for i, (b, queries) in enumerate(pieces):
+            weigh(i, b, queries)
+        for i, (b, queries) in enumerate(pieces):
+            quantise_weights(i, b, queries)
         nc.vector.reciprocal(inv_sum[:], row_sum[:])
 
         for b in range(QB):

from contextlib import ExitStack

import concourse.mybir as mybir
from concourse.masks import make_identity

D, NQ, N, T, DV = 512, 256, 512, 1024, 128
FLOPS = 2 * NQ * N * D + 2 * NQ * N * DV

F32 = mybir.dt.float32
BF16 = mybir.dt.bfloat16
I32 = mybir.dt.int32
U32 = mybir.dt.uint32
U16 = mybir.dt.uint16
U8 = mybir.dt.uint8
FP8X4 = mybir.dt.float8_e4m3fn_x4
ALU = mybir.AluOpType
ACT = mybir.ActivationFunctionType
AX = mybir.AxisListType

P = 128
PACK = 4
QB = NQ // P
EARLY = 512
KB_SCALAR = 192
KB_FIRST = 192
PREFIX = T - N // 2
RUN = 8


def tile_attend_soft_kb_srtq256n512t1024_kernel(tc, qT, k_words, k_scales, vT, vs, kb, offs, out):
    nc = tc.nc
    with ExitStack() as ctx:
        sb = ctx.enter_context(tc.tile_pool(name="sb", bufs=1))
        reuse = ctx.enter_context(tc.tile_pool(name="reuse", bufs=1))
        ps = ctx.enter_context(tc.psum_pool(name="ps", bufs=1))

        def sbuf(name, shape, dtype, tag=None):
            return sb.tile(shape, dtype, name=name, tag=tag or name, align_bytes=64)

        def shared(name, shape, dtype, offset):
            return reuse.tile(shape, dtype, name=name, align_bytes=64, offset=offset)

        def cols(b):
            return slice(b * P, (b + 1) * P)

        halves = [slice(0, T // 2), slice(T // 2, T)]
        offsets = sb.tile([P, N // 16], U16, name="offsets")
        staged = sbuf("staged", [P, PACK * NQ + KB_SCALAR], F32)
        q_raw = staged[:, : PACK * NQ].rearrange("p (j q) -> p j q", j=PACK)
        kb_g = staged[:, PACK * NQ + KB_SCALAR - N :]
        v_k = kb_g[:, : N // 2]
        kw_pool = sbuf("kw_pool", [P, T], I32)
        ks_pool = sbuf("ks_pool", [P, T // 4], I32)
        kb_pool = sbuf("kb_pool", [P, T], F32)
        v_pool = sbuf("v_pool", [P, T], F32, tag="v_pool_then_p0")
        vs_pool = sbuf("vs_pool", [P, T], F32)

        nc.vector.memset(ks_pool[:], 0)
        nc.vector.memset(vs_pool[0 : P - 1, :].bitcast(I32), 0)

        nc.sync.dma_start(offsets[:], offs)
        nc.sync.dma_start(vs_pool[P - 1 : P, :], vs[0:1, :])
        words_hbm = k_words[0].rearrange("p n t -> p (n t)").bitcast(I32)
        nc.sync.dma_start(kw_pool[:, :EARLY], words_hbm[:, :EARLY])
        for quad in range(4):
            queue = nc.sync if quad < 2 else nc.scalar
            queue.dma_start(ks_pool[32 * quad : 32 * quad + 4, :], k_scales[0, 4 * quad : 4 * quad + 4, :].bitcast(I32))
        nc.sync.dma_start(q_raw, qT[0].rearrange("(p j) q -> p j q", j=PACK))
        nc.sync.dma_start(kw_pool[:, EARLY:], words_hbm[:, EARLY:])
        nc.sync.dma_start(kb_pool[:], kb)
        for half in halves:
            nc.sync.dma_start(v_pool[:, half], vT[:, half])

        vs_g = sbuf("vs_g", [P, N], F32)
        nc.vector.tensor_copy(vs_g[:].rearrange("p (m r u e) -> p m u r e", r=RUN // 2, u=2, e=2), vs_pool[:].indirect(offsets[:]))
        ks_g = sbuf("ks_g", [P, N], U8)
        nc.vector.tensor_copy(ks_g[:], ks_pool[:].bitcast(U8).indirect(offsets[:]))
        vs_col = sbuf("vs_col", [P, PACK], F32)
        nc.sync.dma_start(vs_col[:], vs_g[P - 1 : P, :])

        q_bf = [sbuf(f"q_bf{b}", [P, P, PACK], BF16) for b in range(QB)]
        q_codes = [sbuf("q_codes0", [P, P], U32), shared("q_codes1", [P, P], U32, 4096)]
        q_scales = sbuf("q_scales", [P, NQ], U8)
        kw_g = sbuf("kw_g", [P, N], U32)

        def quantise_queries(b):
            nc.vector.quantize_mx(
                out=q_codes[b][:].bitcast(FP8X4),
                scales=q_scales[:, cols(b)],
                in_=q_bf[b][:].rearrange("p q j -> p (q j)"),
            )

        for b in range(QB):
            nc.scalar.activation(
                q_bf[b][:].rearrange("p (c i) j -> p c j i", i=4),
                q_raw[:, :, cols(b)].rearrange("p j (c i) -> p c j i", i=4),
                ACT.Copy,
            )
        quantise_queries(0)
        nc.vector.tensor_copy(kw_g[:], kw_pool[:].bitcast(U32).indirect(offsets[:]))
        quantise_queries(1)
        split = N - KB_SCALAR
        nc.scalar.activation(kb_g[:, split:], kb_pool[:].indirect(offsets[:, split // 16 :]), ACT.Copy)
        for first, last in ((0, KB_FIRST), (KB_FIRST, split)):
            nc.vector.tensor_copy(kb_g[:, first:last], kb_pool[:].indirect(offsets[:, first // 16 : last // 16]))

        ident = sbuf("ident", [P, P], F32, tag="kb_pool")
        make_identity(nc, ident[:])

        score_ps = [[ps.tile([P, N // 2], F32, name=f"score_ps{b}{h}") for h in range(2)] for b in range(QB)]
        for b in range(QB):
            for h in range(2):
                slots = slice(h * N // 2, (h + 1) * N // 2)
                nc.tensor.matmul_mx(
                    out=score_ps[b][h][:],
                    lhsT=q_codes[b][:].bitcast(FP8X4),
                    lhsT_scale=q_scales[:, cols(b)],
                    rhs=kw_g[:, slots].bitcast(FP8X4),
                    rhs_scale=ks_g[:, slots],
                    start=True,
                    stop=True,
                )

        v_bf = sbuf("v_bf", [P, T], BF16)
        for first, last in ((0, T // 2), (T // 2, T - 3 * N // 4), (T - 3 * N // 4, PREFIX)):
            nc.scalar.copy(v_bf[:, first:last], v_pool[:, first:last])
        nc.gpsimd.tensor_copy(v_bf[:, PREFIX:], v_pool[:, PREFIX:])
        v_g = sbuf("v_g", [P, N], BF16)
        for first, last in ((0, N // 4), (N // 4, N // 2), (N // 2, N)):
            runs = v_g[:].rearrange("p (u m x) -> p m u x", u=2, x=RUN)[:, first // 16 : last // 16]
            window = v_bf[:, : T - N + last]
            nc.scalar.activation(runs, window.indirect(offsets[:, first // 16 : last // 16]), ACT.Copy)
        v_ps = ps.tile([P, 2, P], F32, name="v_ps")
        v_words = v_g[:].bitcast(F32)
        for u in range(2):
            nc.tensor.transpose(v_ps[:, u, :], v_words[:, cols(u)], ident[:])

        s_both = sbuf("s_both", [P, QB * N], F32)
        s = [s_both[:, b * N : (b + 1) * N] for b in range(QB)]
        neg_max = [shared("neg_max0", [P, 1], F32, 4096), sbuf("neg_max1", [P, 1], F32)]
        for b in range(QB):
            cuts = [0, KB_FIRST, N // 2, N] if b == 0 else [0, N // 2, N]
            for first, last in zip(cuts, cuts[1:]):
                h, start = divmod(first, N // 2)
                scores = score_ps[b][h][:, start : start + last - first]
                nc.vector.tensor_tensor(s[b][:, first:last], scores, kb_g[:, first:last], ALU.add)
        for b in range(QB):
            nc.vector.tensor_reduce(neg_max[b][:], s[b], AX.X, ALU.max, negate=True)
        features = [slice(0, DV // 2), slice(DV // 2, DV)]
        for part in features:
            nc.vector.tensor_copy(
                v_k.rearrange("p (e u) -> p e u", u=2)[:, part], v_ps[:, :, part].rearrange("p u e -> p e u")
            )
        v_codes = sbuf("v_codes", [P, DV], U32)
        v_scales = sbuf("v_scales", [P, DV], U8)
        for part in features:
            nc.vector.quantize_mx(
                out=v_codes[:, part].bitcast(FP8X4),
                scales=v_scales[:, part],
                in_=v_k[:, 2 * part.start : 2 * part.stop].bitcast(BF16),
            )

        p = [sbuf("p0", [P, PACK, P], F32, tag="v_pool_then_p0"), sbuf("p1", [P, PACK, P], F32)]
        p_ps = [ps.tile([P, PACK, P], F32, name=f"p_ps{b}") for b in range(QB)]
        for b in range(QB):
            for t in range(PACK):
                nc.scalar.activation(
                    p[b][:, t, :].rearrange("p (m r) -> p m r", r=RUN // 2),
                    s[b].rearrange("p (m u r e) -> p u e m r", u=2, r=RUN // 2, e=2)[:, t // 2, t % 2],
                    ACT.Exp,
                    bias=neg_max[b][:],
                )
                nc.tensor.transpose(p_ps[b][:, t, :], p[b][:, t, :], ident[:])

        row_sum = sbuf("row_sum", [P, QB], F32)
        for b in range(QB):
            nc.scalar.activation(
                s_both[:].rearrange("p (m u x) -> p u m x", u=2, x=RUN)[:, b],
                p[b][:].rearrange("p t (m x) -> p (t m) x", x=RUN),
                ACT.Copy,
                accum_out=row_sum[:, b : b + 1],
            )

        pieces = [(0, slice(0, P)), (1, slice(0, P // 2)), (1, slice(P // 2, P))]
        w = [sbuf(f"w{i}", [P, queries.stop - queries.start, PACK], BF16) for i, (b, queries) in enumerate(pieces)]
        w_codes = [sbuf(f"w_codes{b}", [P, P], U32) for b in range(QB)]
        w_scales = [sbuf(f"w_scales{b}", [P, P], U8) for b in range(QB)]
        inv_sum = sbuf("inv_sum", [P, QB], F32, tag="w1")

        def weigh(i, b, queries):
            nc.vector.tensor_tensor(
                w[i][:],
                p_ps[b][:, :, queries].rearrange("p t q -> p q t"),
                vs_col[:].unsqueeze(1).to_broadcast([P, queries.stop - queries.start, PACK]),
                ALU.mult,
            )

        def quantise_weights(i, b, queries):
            nc.vector.quantize_mx(
                out=w_codes[b][:, queries].bitcast(FP8X4),
                scales=w_scales[b][:, queries],
                in_=w[i][:].rearrange("p q t -> p (q t)"),
            )

        for i, (b, queries) in enumerate(pieces):
            weigh(i, b, queries)
        for i, (b, queries) in enumerate(pieces):
            quantise_weights(i, b, queries)
        nc.vector.reciprocal(inv_sum[:], row_sum[:])

        for b in range(QB):
            y_ps = ps.tile([P, DV], F32, name=f"y_ps{b}", tag=f"score_ps{b}0")
            nc.tensor.matmul_mx(
                out=y_ps[:],
                lhsT=w_codes[b][:].bitcast(FP8X4),
                lhsT_scale=w_scales[b][:],
                rhs=v_codes[:].bitcast(FP8X4),
                rhs_scale=v_scales[:],
                start=True,
                stop=True,
            )
            y = sbuf(f"y{b}", [P, DV], F32)
            nc.vector.tensor_scalar(y[:], y_ps[:], inv_sum[:, b : b + 1], None, ALU.mult)
            nc.sync.dma_start(out[0, cols(b), :], y[:])
